import numpy as np
import ml_dtypes


def mxq(x, axis, fmt="e4m3"):
    dtype, down = {"e4m3": (ml_dtypes.float8_e4m3fn, 7), "e5m2": (ml_dtypes.float8_e5m2, 14)}[fmt]
    v = np.moveaxis(np.asarray(x, np.float32).astype(ml_dtypes.bfloat16).astype(np.float64), axis, -1)
    blocks = v.reshape(v.shape[:-1] + (-1, 32))
    amax = np.abs(blocks).max(-1, keepdims=True)
    byte = np.maximum(np.where(amax > 0, np.frexp(amax)[1] - 1 + 127, 0) - down, 1)
    scale = np.exp2(byte - 127.0)
    codes = (blocks / scale).astype(np.float32).astype(dtype).astype(np.float64)
    return np.moveaxis((codes * scale).reshape(v.shape), -1, axis)


WIDE = False


def mx_kscale(k):
    if not WIDE:
        return np.ones(k)
    levels = np.array([24, -24, 12, -12, 0])
    if k % 512:
        return np.exp2(np.random.permutation(np.resize(levels, k // 32))).repeat(32)
    a = np.empty((k // 512, 16))
    for p in range(k // 512):
        a[p, :8] = np.random.permutation(np.resize(levels, 8))
        for g in range(8):
            far = levels[np.abs(levels - a[p, g]) >= 10]
            a[p, g + 8] = far[np.random.randint(len(far))]
    return np.exp2(a.ravel()).repeat(32)


def f64(x):
    return np.asarray(x).astype(np.float64)


def striped(idx):
    return np.tile(idx.reshape(-1, 16).T, (8, 1)).astype(np.uint16)


def unstriped(offs):
    return offs[:16].T.reshape(-1).astype(np.int64)


E2M1 = np.array([0.0, 0.5, 1.0, 1.5, 2.0, 3.0, 4.0, 6.0, -0.0, -0.5, -1.0, -1.5, -2.0, -3.0, -4.0, -6.0])


def pack_weight(w, fmt):
    k, n = w.shape
    w = f64(np.asarray(w, np.float32).astype(ml_dtypes.bfloat16)).reshape(k // 32, 32, n)
    amax = np.abs(w).max(1)
    if fmt == "e4m3":
        byte = np.frexp(amax)[1] - 1 + 127 - 7
    else:
        mant, ex = np.frexp(amax / 6.0)
        byte = np.where(mant > 0.5, ex, ex - 1) + 127
    byte = np.clip(np.where(amax > 0, byte, 1), 1, 254)
    scaled = (w * np.exp2(127.0 - byte)[:, None, :]).reshape(k, n).astype(np.float32)
    by_word = np.ascontiguousarray(scaled.reshape(k // 512, 128, 4, n).transpose(0, 1, 3, 2))
    if fmt == "e4m3":
        words = by_word.astype(ml_dtypes.float8_e4m3fn).view(np.uint8)
    else:
        c = by_word.astype(ml_dtypes.float4_e2m1fn).view(np.uint8) & 0xF
        words = (c[..., 0::2] | (c[..., 1::2] << 4)).reshape(k // 512, 128, 2 * n)
    return np.ascontiguousarray(words), np.ascontiguousarray(byte.astype(np.uint8).reshape(k // 512, 16, n))


def unpack_weight(words, scales, fmt):
    g, _, n = scales.shape
    words = np.ascontiguousarray(words).reshape(g, 128, n, -1)
    if fmt == "e4m3":
        vals = words.view(ml_dtypes.float8_e4m3fn).astype(np.float64)
    else:
        nib = np.empty((g, 128, n, 4), np.uint8)
        nib[..., 0::2] = words & 0xF
        nib[..., 1::2] = words >> 4
        vals = E2M1[nib]
    vals = vals * np.repeat(np.exp2(scales.astype(np.float64) - 127.0), 8, axis=1)[..., None]
    return vals.transpose(0, 1, 3, 2).reshape(g * 512, n)


def sigm(f):
    return 1.0 / (1.0 + np.exp(-np.maximum(f, -700.0)))


K, L, R, N, T, J = 512, 512, 1024, 1024, 4096, 1024


def setup_inputs():
    n = np.random.standard_normal
    s = mx_kscale(K)[:, None]
    s2 = mx_kscale(L)[:, None]
    u = mx_kscale(R)[:, None]
    p_tab = pack_weight(n((K, T)) * s, "e4m3")
    p_tab2 = pack_weight(n((L, T)) * s2, "e4m3")
    p_wa = pack_weight(n((K, R)) / np.sqrt(K) / s * u.T, "e4m3")
    p_en = pack_weight(n((R, N)) / np.sqrt(R) / u, "e4m3")
    return {
        "tab_words": p_tab[0],
        "tab_scales": p_tab[1],
        "tab2_words": p_tab2[0],
        "tab2_scales": p_tab2[1],
        "wa_words": p_wa[0],
        "wa_scales": p_wa[1],
        "wb": (n((L, R)) / np.sqrt(L) / s2).astype(np.float32),
        "en_words": p_en[0],
        "en_scales": p_en[1],
        "offs": striped(np.random.permutation(T)[:J]),
        "offs2": striped(np.random.permutation(T)[:J]),
    }


def reference(tab_words, tab_scales, tab2_words, tab2_scales, wa_words, wa_scales, wb, en_words, en_scales, offs, offs2):
    idx = unstriped(offs)
    idx2 = unstriped(offs2)
    tab_ = unpack_weight(tab_words, tab_scales, "e4m3")[:, idx]
    tab2_ = unpack_weight(tab2_words, tab2_scales, "e4m3")[:, idx2]
    wa_ = unpack_weight(wa_words, wa_scales, "e4m3")
    wb_ = mxq(f64(wb), 0, "e4m3")
    ha = wa_.T @ tab_
    hb = wb_.T @ tab2_
    h = ha * hb
    h_ = mxq(h, 0, "e4m3")
    en_ = unpack_weight(en_words, en_scales, "e4m3")
    y = en_.T @ h_
    return sigm(y)

@@ -1,0 +1,229 @@
+from contextlib import ExitStack
+
+import concourse.mybir as mybir
+
+K, L, R, N, T, J = 512, 512, 1024, 1024, 4096, 1024
+FLOPS = 2 * J * (K * R + L * R + R * N)
+
+F32 = mybir.dt.float32
+BF16 = mybir.dt.bfloat16
+I32 = mybir.dt.int32
+U32 = mybir.dt.uint32
+U16 = mybir.dt.uint16
+U8 = mybir.dt.uint8
+FP8X4 = mybir.dt.float8_e4m3fn_x4
+MULT = mybir.AluOpType.mult
+SIGMOID = mybir.ActivationFunctionType.Sigmoid
+
+P = 128
+PACK = 4
+PASS = P * PACK
+R_PASSES = R // PASS
+HALF = 512
+PIECE = 128
+CHUNKS = [128, 256, 256, 256, 128]
+TAB_FIRST = 1024
+TAB_ROW, TAB2_ROW, WA_ROW, EN_ROW = 0, 4, 0, 8
+
+
+def as_words(words):
+    return words.rearrange("p n i -> p (n i)").bitcast(I32)
+
+
+def load_scale_rows(queue, plane, first_row, scales):
+    by_row = scales.rearrange("a (q r) n -> r q a n", r=PACK)
+    for r in range(PACK):
+        queue.dma_start(out=plane[first_row + r : P : 32], in_=by_row[r].bitcast(I32))
+
+
+def tile_list_kg_mul_sig_kernel(
+    tc, tab_words, tab_scales, tab2_words, tab2_scales, wa_words, wa_scales, wb, en_words, en_scales, offs, offs2, out
+):
+    nc = tc.nc
+    with ExitStack() as ctx:
+        keep = ctx.enter_context(tc.tile_pool(name="keep", bufs=1))
+        reuse = ctx.enter_context(tc.tile_pool(name="reuse", bufs=1))
+        stage = ctx.enter_context(tc.tile_pool(name="stage", bufs=8))
+        psum_s = ctx.enter_context(tc.psum_pool(name="psum_s", bufs=4))
+        psum_v = ctx.enter_context(tc.psum_pool(name="psum_v", bufs=4))
+
+        list_a = keep.tile([P, J // 16], U16, name="list_a")
+        list_b = keep.tile([P, J // 16], U16, name="list_b")
+        tab_w = reuse.tile([P, T], I32, name="tab_w", tag="slot_a", align_bytes=64)
+        tab_s = reuse.tile([P, 1, T // 4], I32, name="tab_s", tag="slot_b", align_bytes=64)
+        tab2_s = reuse.tile([P, 1, T // 4], I32, name="tab2_s", tag="slot_e", align_bytes=64)
+        wa_raw_w = reuse.tile([P, R], I32, name="wa_raw_w", tag="slot_c", align_bytes=64)
+        wa_raw_s = reuse.tile([P, R // 4], I32, name="wa_raw_s", tag="slot_d", align_bytes=64)
+
+        nc.vector.memset(tab_s[:], 0)
+        nc.vector.memset(tab2_s[:], 0)
+
+        warm_in = keep.tile([P, 1], F32, name="warm_in")
+        warm_out = keep.tile([P, 1], F32, name="warm_out")
+        nc.vector.memset(warm_in[:], 0.0)
+        nc.scalar.activation(warm_out[:], warm_in[:], SIGMOID)
+
+        for q in range(4):
+            rows = wa_scales[0, 4 * q : 4 * q + 4, :].bitcast(I32)
+            nc.sync.dma_start(out=wa_raw_s[32 * q : 32 * q + 32, :], in_=rows.unsqueeze(0).to_broadcast([8, 4, R // 4]))
+        nc.sync.dma_start(list_a[:], offs)
+        nc.sync.dma_start(list_b[:], offs2)
+        nc.sync.dma_start(out=wa_raw_w[:], in_=as_words(wa_words[0]))
+        nc.sync.dma_start(out=tab_w[:, :TAB_FIRST], in_=as_words(tab_words[0])[:, :TAB_FIRST])
+        load_scale_rows(nc.sync, tab_s, TAB_ROW, tab_scales)
+        nc.sync.dma_start(out=tab_w[:, TAB_FIRST:], in_=as_words(tab_words[0])[:, TAB_FIRST:])
+        load_scale_rows(nc.sync, tab2_s, TAB2_ROW, tab2_scales)
+
+        va_w = keep.tile([P, J], U32, name="va_w", align_bytes=64)
+        va_s = keep.tile([P, J], U8, name="va_s", align_bytes=64)
+        vb_w = keep.tile([P, J], U32, name="vb_w", align_bytes=64)
+        vb_s = keep.tile([P, J], U8, name="vb_s", align_bytes=64)
+
+        def gather_words(words, table_w, offsets, half):
+            cols = slice(half * HALF, (half + 1) * HALF)
+            entries = offsets[:, half * HALF // 16 : (half + 1) * HALF // 16]
+            nc.vector.tensor_copy(words[:, cols], table_w[:].bitcast(U32).indirect(entries))
+
+        def gather_scales(scales, table_s, offsets):
+            plane = table_s[:].rearrange("p a t -> p (a t)").bitcast(U8)
+            nc.vector.tensor_copy(scales[:], plane.indirect(offsets[:]))
+
+        wa_w = keep.tile([P, R], I32, name="wa_w", align_bytes=64)
+        wa_s = keep.tile([P, R], U8, name="wa_s", align_bytes=64)
+        wa_raw_bytes = wa_raw_s[:].bitcast(U8)
+
+        def reorder_wa_words(a):
+            cols = slice(a * PASS, (a + 1) * PASS)
+            nc.vector.tensor_copy(
+                out=wa_w[:, cols].rearrange("p (t g m) -> p g t m", t=PACK, m=4),
+                in_=wa_raw_w[:, cols].rearrange("p (g m t) -> p g t m", t=PACK, m=4),
+            )
+
+        def reorder_wa_scales(a):
+            cols = slice(a * PASS, (a + 1) * PASS)
+            nc.vector.tensor_copy(
+                out=wa_s[:, cols].rearrange("p (t m) -> p m t", t=PACK),
+                in_=wa_raw_bytes[:, cols].rearrange("p (m t) -> p m t", t=PACK),
+            )
+
+        def project(bank, w_words, w_scales, w_row, v_words, v_scales, v_row, a, j0):
+            for t in range(PACK):
+                r_cols = slice(a * PASS + t * P, a * PASS + (t + 1) * P)
+                nc.tensor.matmul_mx(
+                    out=bank[:, t, :],
+                    lhsT=w_words[:, r_cols].bitcast(FP8X4),
+                    lhsT_scale=w_scales[w_row:P, r_cols],
+                    rhs=v_words[:, j0 : j0 + PIECE].bitcast(FP8X4),
+                    rhs_scale=v_scales[v_row:P, j0 : j0 + PIECE],
+                    start=True,
+                    stop=True,
+                )
+
+        ha = {}
+
+        def make_ha(tile, start, stop):
+            for j0 in range(start, stop, PIECE):
+                for a in range(R_PASSES):
+                    ha[a, j0] = tile[:, (j0 - start) // PIECE, a]
+                    bank = psum_s.tile([P, PACK, PIECE], F32, name="bank_s")
+                    project(bank, wa_w, wa_s, WA_ROW, va_w, va_s, TAB_ROW, a, j0)
+                    nc.scalar.copy(out=ha[a, j0], in_=bank[:].rearrange("p t j -> p j t"))
+
+        for a in range(R_PASSES):
+            reorder_wa_scales(a)
+        tab2_w = reuse.tile([P, T], I32, name="tab2_w", tag="slot_d", align_bytes=64)
+        nc.sync.dma_start(out=tab2_w[:], in_=as_words(tab2_words[0]))
+        for a in range(R_PASSES):
+            reorder_wa_words(a)
+        wb_rows = wb.rearrange("(p i) r -> p i r", i=PACK)
+        wb_raw = [reuse.tile([P, PACK, PASS], F32, name="wb_raw0", tag="slot_c", align_bytes=64)]
+        nc.sync.dma_start(out=wb_raw[0][:], in_=wb_rows[:, :, :PASS])
+
+        gather_scales(va_s, tab_s, list_a)
+        wb_raw.append(reuse.tile([P, PACK, PASS], F32, name="wb_raw1", tag="slot_b", align_bytes=64))
+        nc.sync.dma_start(out=wb_raw[1][:], in_=wb_rows[:, :, PASS:])
+        for half in range(2):
+            gather_words(va_w, tab_w, list_a, half)
+        en_s = reuse.tile([P, R_PASSES, N // 4], I32, name="en_s", tag="slot_a", align_bytes=64)
+        nc.vector.memset(en_s[:], 0)
+        load_scale_rows(nc.sync, en_s, EN_ROW, en_scales)
+        gather_scales(vb_s, tab2_s, list_b)
+        en_w = reuse.tile([P, R_PASSES, N], I32, name="en_w", tag="slot_e", align_bytes=64)
+        en_view = en_words.rearrange("a p n i -> p a (n i)").bitcast(I32)
+        for n0 in range(0, N, N // 2):
+            nc.sync.dma_start(out=en_w[:, :, n0 : n0 + N // 2], in_=en_view[:, :, n0 : n0 + N // 2])
+        for half in range(2):
+            gather_words(vb_w, tab2_w, list_b, half)
+        ha_first = keep.tile([P, HALF // PIECE, R_PASSES, PIECE, PACK], F32, name="ha_first", align_bytes=64)
+        make_ha(ha_first, 0, HALF)
+
+        wb_w = keep.tile([P, R], U32, name="wb_w", align_bytes=64)
+        wb_s = keep.tile([P, R], U8, name="wb_s", align_bytes=64)
+        for a in range(R_PASSES):
+            wb_bf = keep.tile([P, PASS * PACK], BF16, name="wb_bf%d" % a, align_bytes=64)
+            dst = wb_bf[:].rearrange("p (t m i) -> p m t i", t=PACK, i=PACK)
+            src = wb_raw[a][:].rearrange("p i (m t) -> p m t i", t=PACK)
+            for m0 in range(0, P, P // 2):
+                if m0 > 0:
+                    nc.vector.tensor_copy(out=dst[:, m0 : m0 + P // 2], in_=src[:, m0 : m0 + P // 2])
+                else:
+                    nc.scalar.copy(out=dst[:, m0 : m0 + P // 2], in_=src[:, m0 : m0 + P // 2])
+            cols = slice(a * PASS, (a + 1) * PASS)
+            nc.vector.quantize_mx(out=wb_w[:, cols].bitcast(FP8X4), scales=wb_s[:, cols], in_=wb_bf[:])
+
+
+        for slot, start in (("slot_c", HALF), ("slot_b", HALF + 2 * PIECE)):
+            ha_late = reuse.tile([P, 2, R_PASSES, PIECE, PACK], F32, name="ha_late", tag=slot, align_bytes=64)
+            make_ha(ha_late, start, start + 2 * PIECE)
+
+        h_bf = keep.tile([P, R_PASSES, J, PACK], BF16, name="h_bf", align_bytes=64)
+        h_w = keep.tile([P, R_PASSES, J], U32, name="h_w", align_bytes=64)
+        h_s = keep.tile([P, R_PASSES, J], U8, name="h_s", align_bytes=64)
+        en_bytes = en_s[:].bitcast(U8)
+        out_tiles = out.rearrange("(g p) j -> p g j", p=P)
+
+        def make_h(j0, width):
+            cols = slice(j0, j0 + width)
+            for a in range(R_PASSES):
+                for j1 in range(j0, j0 + width, PIECE):
+                    bank = psum_v.tile([P, PACK, PIECE], F32, name="bank_v")
+                    project(bank, wb_w, wb_s, 0, vb_w, vb_s, TAB2_ROW, a, j1)
+                    nc.vector.tensor_tensor(
+                        h_bf[:, a, j1 : j1 + PIECE, :],
+                        bank[:].rearrange("p t j -> p j t"),
+                        ha[a, j1],
+                        MULT,
+                    )
+                nc.vector.quantize_mx(
+                    out=h_w[:, a, cols].bitcast(FP8X4),
+                    scales=h_s[:, a, cols],
+                    in_=h_bf[:, a, cols, :].rearrange("p j t -> p (j t)"),
+                )
+
+        def score(j0, width):
+            cols = slice(j0, j0 + width)
+            groups = PASS // width
+            for g0 in range(0, N // P, groups):
+                bank = psum_s.tile([P, groups, width], F32, name="bank_s")
+                for g in range(groups):
+                    n_cols = slice((g0 + g) * P, (g0 + g + 1) * P)
+                    for a in range(R_PASSES):
+                        nc.tensor.matmul_mx(
+                            out=bank[:, g, :],
+                            lhsT=en_w[:, a, n_cols].bitcast(FP8X4),
+                            lhsT_scale=en_bytes[EN_ROW:P, a, n_cols],
+                            rhs=h_w[:, a, cols].bitcast(FP8X4),
+                            rhs_scale=h_s[:, a, cols],
+                            start=(a == 0),
+                            stop=(a == R_PASSES - 1),
+                        )
+                result = stage.tile([P, groups, width], F32, name="result")
+                nc.scalar.activation(result[:], bank[:], SIGMOID)
+                nc.sync.dma_start(out=out_tiles[:, g0 : g0 + groups, cols], in_=result[:])
+
+        chunks = [(sum(CHUNKS[:c]), CHUNKS[c]) for c in range(len(CHUNKS))]
+        make_h(*chunks[0])
+        for c in range(len(chunks)):
+            if c + 1 < len(chunks):
+                make_h(*chunks[c + 1])
+            score(*chunks[c])

@@ -19,21 +19,27 @@ P = 128
 PACK = 4
 PASS = P * PACK
 R_PASSES = R // PASS
-HALF = 512
-PIECE = 128
+QUADRANT = 32
+LIST_GROUP = 16
+HALF = J // 2
+PIECE = P
+BANK = 512
+BANKS = 8
+HA_BANKS = 4
 CHUNKS = [128, 256, 256, 256, 128]
-TAB_FIRST = 1024
+TAB_FIRST = 768
 TAB_ROW, TAB2_ROW, WA_ROW, EN_ROW = 0, 4, 0, 8
+STORES = J * N // (P * BANK)
 
 
-def as_words(words):
-    return words.rearrange("p n i -> p (n i)").bitcast(I32)
+def as_words(codes):
+    return codes.rearrange("p n i -> p (n i)").bitcast(I32)
 
 
-def load_scale_rows(queue, plane, first_row, scales):
+def load_scale_rows(nc, plane, first_row, scales):
     by_row = scales.rearrange("a (q r) n -> r q a n", r=PACK)
     for r in range(PACK):
-        queue.dma_start(out=plane[first_row + r : P : 32], in_=by_row[r].bitcast(I32))
+        nc.sync.dma_start(out=plane[first_row + r : P : QUADRANT], in_=by_row[r].bitcast(I32))
 
 
 def tile_list_kg_mul_sig_kernel(
@@ -43,17 +49,16 @@ def tile_list_kg_mul_sig_kernel(
     with ExitStack() as ctx:
         keep = ctx.enter_context(tc.tile_pool(name="keep", bufs=1))
         reuse = ctx.enter_context(tc.tile_pool(name="reuse", bufs=1))
-        stage = ctx.enter_context(tc.tile_pool(name="stage", bufs=8))
-        psum_s = ctx.enter_context(tc.psum_pool(name="psum_s", bufs=4))
-        psum_v = ctx.enter_context(tc.psum_pool(name="psum_v", bufs=4))
+        stage = ctx.enter_context(tc.tile_pool(name="stage", bufs=STORES))
+        psum = ctx.enter_context(tc.psum_pool(name="psum", bufs=1))
 
-        list_a = keep.tile([P, J // 16], U16, name="list_a")
-        list_b = keep.tile([P, J // 16], U16, name="list_b")
-        tab_w = reuse.tile([P, T], I32, name="tab_w", tag="slot_a", align_bytes=64)
-        tab_s = reuse.tile([P, 1, T // 4], I32, name="tab_s", tag="slot_b", align_bytes=64)
-        tab2_s = reuse.tile([P, 1, T // 4], I32, name="tab2_s", tag="slot_e", align_bytes=64)
-        wa_raw_w = reuse.tile([P, R], I32, name="wa_raw_w", tag="slot_c", align_bytes=64)
-        wa_raw_s = reuse.tile([P, R // 4], I32, name="wa_raw_s", tag="slot_d", align_bytes=64)
+        list_a = keep.tile([P, J // LIST_GROUP], U16, name="list_a")
+        list_b = keep.tile([P, J // LIST_GROUP], U16, name="list_b")
+        tab_s = keep.tile([P, 1, T // 4], I32, name="tab_s", align_bytes=64)
+        tab2_s = reuse.tile([P, 1, T // 4], I32, name="tab2_s", tag="tab2_s_en_s", align_bytes=64)
+        wa_raw_w = reuse.tile([P, R], I32, name="wa_raw_w", tag="wa_w_tab2_w", align_bytes=64)
+        wa_raw_s = reuse.tile([P, R // 4], I32, name="wa_raw_s", tag="wa_s_wb", align_bytes=64)
+        tab_w = reuse.tile([P, T], I32, name="tab_w", tag="tab_w_en_w", align_bytes=64)
 
         nc.vector.memset(tab_s[:], 0)
         nc.vector.memset(tab2_s[:], 0)
@@ -63,48 +68,75 @@ def tile_list_kg_mul_sig_kernel(
         nc.vector.memset(warm_in[:], 0.0)
         nc.scalar.activation(warm_out[:], warm_in[:], SIGMOID)
 
-        for q in range(4):
-            rows = wa_scales[0, 4 * q : 4 * q + 4, :].bitcast(I32)
-            nc.sync.dma_start(out=wa_raw_s[32 * q : 32 * q + 32, :], in_=rows.unsqueeze(0).to_broadcast([8, 4, R // 4]))
+        for q in range(P // QUADRANT):
+            rows = wa_scales[0, PACK * q : PACK * (q + 1), :].bitcast(I32)
+            nc.sync.dma_start(
+                out=wa_raw_s[QUADRANT * q : QUADRANT * (q + 1), :],
+                in_=rows.unsqueeze(0).to_broadcast([QUADRANT // PACK, PACK, R // 4]),
+            )
         nc.sync.dma_start(list_a[:], offs)
         nc.sync.dma_start(list_b[:], offs2)
         nc.sync.dma_start(out=wa_raw_w[:], in_=as_words(wa_words[0]))
         nc.sync.dma_start(out=tab_w[:, :TAB_FIRST], in_=as_words(tab_words[0])[:, :TAB_FIRST])
-        load_scale_rows(nc.sync, tab_s, TAB_ROW, tab_scales)
+        load_scale_rows(nc, tab_s, TAB_ROW, tab_scales)
+        load_scale_rows(nc, tab2_s, TAB2_ROW, tab2_scales)
         nc.sync.dma_start(out=tab_w[:, TAB_FIRST:], in_=as_words(tab_words[0])[:, TAB_FIRST:])
-        load_scale_rows(nc.sync, tab2_s, TAB2_ROW, tab2_scales)
-
-        va_w = keep.tile([P, J], U32, name="va_w", align_bytes=64)
-        va_s = keep.tile([P, J], U8, name="va_s", align_bytes=64)
-        vb_w = keep.tile([P, J], U32, name="vb_w", align_bytes=64)
-        vb_s = keep.tile([P, J], U8, name="vb_s", align_bytes=64)
-
-        def gather_words(words, table_w, offsets, half):
-            cols = slice(half * HALF, (half + 1) * HALF)
-            entries = offsets[:, half * HALF // 16 : (half + 1) * HALF // 16]
-            nc.vector.tensor_copy(words[:, cols], table_w[:].bitcast(U32).indirect(entries))
-
-        def gather_scales(scales, table_s, offsets):
-            plane = table_s[:].rearrange("p a t -> p (a t)").bitcast(U8)
-            nc.vector.tensor_copy(scales[:], plane.indirect(offsets[:]))
 
         wa_w = keep.tile([P, R], I32, name="wa_w", align_bytes=64)
         wa_s = keep.tile([P, R], U8, name="wa_s", align_bytes=64)
-        wa_raw_bytes = wa_raw_s[:].bitcast(U8)
-
-        def reorder_wa_words(a):
-            cols = slice(a * PASS, (a + 1) * PASS)
+        passes = [slice(a * PASS, (a + 1) * PASS) for a in range(R_PASSES)]
+        for cols in passes:
             nc.vector.tensor_copy(
-                out=wa_w[:, cols].rearrange("p (t g m) -> p g t m", t=PACK, m=4),
-                in_=wa_raw_w[:, cols].rearrange("p (g m t) -> p g t m", t=PACK, m=4),
+                out=wa_s[:, cols].rearrange("p (t m) -> p t m", t=PACK),
+                in_=wa_raw_s[:].bitcast(U8)[:, cols].rearrange("p (m t) -> p t m", t=PACK),
             )
-
-        def reorder_wa_scales(a):
-            cols = slice(a * PASS, (a + 1) * PASS)
+        wb_raw = reuse.tile([P, R_PASSES, PACK, PASS], F32, name="wb_raw", tag="wa_s_wb", align_bytes=64)
+        wb_rows = wb.rearrange("(p i) r -> p i r", i=PACK)
+        for a, cols in enumerate(passes):
+            nc.sync.dma_start(out=wb_raw[:, a], in_=wb_rows[:, :, cols])
+        for cols in passes:
             nc.vector.tensor_copy(
-                out=wa_s[:, cols].rearrange("p (t m) -> p m t", t=PACK),
-                in_=wa_raw_bytes[:, cols].rearrange("p (m t) -> p m t", t=PACK),
+                out=wa_w[:, cols].rearrange("p (t g u) -> p g t u", t=PACK, u=4),
+                in_=wa_raw_w[:, cols].rearrange("p (g u t) -> p g t u", t=PACK, u=4),
             )
+        tab2_w = reuse.tile([P, T], I32, name="tab2_w", tag="wa_w_tab2_w", align_bytes=64)
+        nc.sync.dma_start(out=tab2_w[:], in_=as_words(tab2_words[0]))
+
+        va_w = [keep.tile([P, HALF], U32, name="va_w%d" % half, align_bytes=64) for half in range(2)]
+        vb_w = [keep.tile([P, HALF], U32, name="vb_w%d" % half, align_bytes=64) for half in range(2)]
+        va_s = keep.tile([P, J], U8, name="va_s", align_bytes=64)
+        vb_s = keep.tile([P, J], U8, name="vb_s", align_bytes=64)
+
+        def gather_scales(picked, plane, offsets):
+            window = plane[:].rearrange("p a t -> p (a t)").bitcast(U8)
+            nc.vector.tensor_copy(picked[:], window.indirect(offsets[:]))
+
+        def gather_words(picked, table, offsets):
+            for half in range(2):
+                entries = offsets[:, half * HALF // LIST_GROUP : (half + 1) * HALF // LIST_GROUP]
+                nc.vector.tensor_copy(picked[half][:], table[:].bitcast(U32).indirect(entries))
+
+        gather_scales(va_s, tab_s, list_a)
+        gather_scales(vb_s, tab2_s, list_b)
+        en_s = reuse.tile([P, R_PASSES, N // 4], I32, name="en_s", tag="tab2_s_en_s", align_bytes=64)
+        nc.vector.memset(en_s[:], 0)
+        load_scale_rows(nc, en_s, EN_ROW, en_scales)
+        gather_words(va_w, tab_w, list_a)
+        en_w = reuse.tile([P, R_PASSES, N], I32, name="en_w", tag="tab_w_en_w", align_bytes=64)
+        en_view = en_words.rearrange("a p n i -> p a (n i)").bitcast(I32)
+        for n0 in range(0, N, N // 2):
+            nc.sync.dma_start(out=en_w[:, :, n0 : n0 + N // 2], in_=en_view[:, :, n0 : n0 + N // 2])
+
+        wb_w = keep.tile([P, R], U32, name="wb_w", align_bytes=64)
+        wb_s = keep.tile([P, R], U8, name="wb_s", align_bytes=64)
+        for a, cols in enumerate(passes):
+            wb_bf = keep.tile([P, PASS * PACK], BF16, name="wb_bf%d" % a, align_bytes=64)
+            nc.vector.tensor_copy(
+                out=wb_bf[:].rearrange("p (t m i) -> p m t i", t=PACK, i=PACK),
+                in_=wb_raw[:, a].rearrange("p i (m t) -> p m t i", t=PACK),
+            )
+            nc.vector.quantize_mx(out=wb_w[:, cols].bitcast(FP8X4), scales=wb_s[:, cols], in_=wb_bf[:])
+        gather_words(vb_w, tab2_w, list_b)
 
         def project(bank, w_words, w_scales, w_row, v_words, v_scales, v_row, a, j0):
             for t in range(PACK):
@@ -113,117 +145,82 @@ def tile_list_kg_mul_sig_kernel(
                     out=bank[:, t, :],
                     lhsT=w_words[:, r_cols].bitcast(FP8X4),
                     lhsT_scale=w_scales[w_row:P, r_cols],
-                    rhs=v_words[:, j0 : j0 + PIECE].bitcast(FP8X4),
+                    rhs=v_words[j0 // HALF][:, j0 % HALF : j0 % HALF + PIECE].bitcast(FP8X4),
                     rhs_scale=v_scales[v_row:P, j0 : j0 + PIECE],
                     start=True,
                     stop=True,
                 )
 
-        ha = {}
+        ha = keep.tile([P, J // PIECE, R_PASSES, PIECE, PACK], F32, name="ha", align_bytes=64)
+        for piece in range(J // PIECE):
+            for a in range(R_PASSES):
+                tag = "bank%d" % ((piece * R_PASSES + a) % HA_BANKS)
+                bank = psum.tile([P, PACK, PIECE], F32, name="ha_bank", tag=tag)
+                project(bank, wa_w, wa_s, WA_ROW, va_w, va_s, TAB_ROW, a, piece * PIECE)
+                nc.scalar.copy(out=ha[:, piece, a], in_=bank[:].rearrange("p t j -> p j t"))
 
-        def make_ha(tile, start, stop):
-            for j0 in range(start, stop, PIECE):
-                for a in range(R_PASSES):
-                    ha[a, j0] = tile[:, (j0 - start) // PIECE, a]
-                    bank = psum_s.tile([P, PACK, PIECE], F32, name="bank_s")
-                    project(bank, wa_w, wa_s, WA_ROW, va_w, va_s, TAB_ROW, a, j0)
-                    nc.scalar.copy(out=ha[a, j0], in_=bank[:].rearrange("p t j -> p j t"))
+        taken = []
 
-        for a in range(R_PASSES):
-            reorder_wa_scales(a)
-        tab2_w = reuse.tile([P, T], I32, name="tab2_w", tag="slot_d", align_bytes=64)
-        nc.sync.dma_start(out=tab2_w[:], in_=as_words(tab2_words[0]))
-        for a in range(R_PASSES):
-            reorder_wa_words(a)
-        wb_rows = wb.rearrange("(p i) r -> p i r", i=PACK)
-        wb_raw = [reuse.tile([P, PACK, PASS], F32, name="wb_raw0", tag="slot_c", align_bytes=64)]
-        nc.sync.dma_start(out=wb_raw[0][:], in_=wb_rows[:, :, :PASS])
+        def take_bank(shape):
+            taken.append(shape)
+            return psum.tile(shape, F32, name="bank", tag="bank%d" % ((HA_BANKS + len(taken) - 1) % BANKS))
 
-        gather_scales(va_s, tab_s, list_a)
-        wb_raw.append(reuse.tile([P, PACK, PASS], F32, name="wb_raw1", tag="slot_b", align_bytes=64))
-        nc.sync.dma_start(out=wb_raw[1][:], in_=wb_rows[:, :, PASS:])
-        for half in range(2):
-            gather_words(va_w, tab_w, list_a, half)
-        en_s = reuse.tile([P, R_PASSES, N // 4], I32, name="en_s", tag="slot_a", align_bytes=64)
-        nc.vector.memset(en_s[:], 0)
-        load_scale_rows(nc.sync, en_s, EN_ROW, en_scales)
-        gather_scales(vb_s, tab2_s, list_b)
-        en_w = reuse.tile([P, R_PASSES, N], I32, name="en_w", tag="slot_e", align_bytes=64)
-        en_view = en_words.rearrange("a p n i -> p a (n i)").bitcast(I32)
-        for n0 in range(0, N, N // 2):
-            nc.sync.dma_start(out=en_w[:, :, n0 : n0 + N // 2], in_=en_view[:, :, n0 : n0 + N // 2])
-        for half in range(2):
-            gather_words(vb_w, tab2_w, list_b, half)
-        ha_first = keep.tile([P, HALF // PIECE, R_PASSES, PIECE, PACK], F32, name="ha_first", align_bytes=64)
-        make_ha(ha_first, 0, HALF)
+        h_bf, h_w, h_s = {}, {}, {}
+        unquantised = []
 
-        wb_w = keep.tile([P, R], U32, name="wb_w", align_bytes=64)
-        wb_s = keep.tile([P, R], U8, name="wb_s", align_bytes=64)
-        for a in range(R_PASSES):
-            wb_bf = keep.tile([P, PASS * PACK], BF16, name="wb_bf%d" % a, align_bytes=64)
-            dst = wb_bf[:].rearrange("p (t m i) -> p m t i", t=PACK, i=PACK)
-            src = wb_raw[a][:].rearrange("p i (m t) -> p m t i", t=PACK)
-            for m0 in range(0, P, P // 2):
-                if m0 > 0:
-                    nc.vector.tensor_copy(out=dst[:, m0 : m0 + P // 2], in_=src[:, m0 : m0 + P // 2])
-                else:
-                    nc.scalar.copy(out=dst[:, m0 : m0 + P // 2], in_=src[:, m0 : m0 + P // 2])
-            cols = slice(a * PASS, (a + 1) * PASS)
-            nc.vector.quantize_mx(out=wb_w[:, cols].bitcast(FP8X4), scales=wb_s[:, cols], in_=wb_bf[:])
-
-
-        for slot, start in (("slot_c", HALF), ("slot_b", HALF + 2 * PIECE)):
-            ha_late = reuse.tile([P, 2, R_PASSES, PIECE, PACK], F32, name="ha_late", tag=slot, align_bytes=64)
-            make_ha(ha_late, start, start + 2 * PIECE)
-
-        h_bf = keep.tile([P, R_PASSES, J, PACK], BF16, name="h_bf", align_bytes=64)
-        h_w = keep.tile([P, R_PASSES, J], U32, name="h_w", align_bytes=64)
-        h_s = keep.tile([P, R_PASSES, J], U8, name="h_s", align_bytes=64)
-        en_bytes = en_s[:].bitcast(U8)
-        out_tiles = out.rearrange("(g p) j -> p g j", p=P)
+        def quantize_h(j0, a):
+            nc.vector.quantize_mx(
+                out=h_w[j0][:, a].bitcast(FP8X4),
+                scales=h_s[j0][:, a],
+                in_=h_bf[j0][:, a].rearrange("p j t -> p (j t)"),
+            )
 
         def make_h(j0, width):
-            cols = slice(j0, j0 + width)
+            h_bf[j0] = keep.tile([P, R_PASSES, width, PACK], BF16, name="h_bf%d" % j0, align_bytes=64)
+            h_w[j0] = keep.tile([P, R_PASSES, width], U32, name="h_w%d" % j0, align_bytes=64)
+            h_s[j0] = keep.tile([P, R_PASSES, width], U8, name="h_s%d" % j0, align_bytes=64)
             for a in range(R_PASSES):
-                for j1 in range(j0, j0 + width, PIECE):
-                    bank = psum_v.tile([P, PACK, PIECE], F32, name="bank_v")
-                    project(bank, wb_w, wb_s, 0, vb_w, vb_s, TAB2_ROW, a, j1)
+                for j1 in range(0, width, PIECE):
+                    bank = take_bank([P, PACK, PIECE])
+                    project(bank, wb_w, wb_s, 0, vb_w, vb_s, TAB2_ROW, a, j0 + j1)
                     nc.vector.tensor_tensor(
-                        h_bf[:, a, j1 : j1 + PIECE, :],
+                        h_bf[j0][:, a, j1 : j1 + PIECE, :],
                         bank[:].rearrange("p t j -> p j t"),
-                        ha[a, j1],
+                        ha[:, (j0 + j1) // PIECE, a],
                         MULT,
                     )
-                nc.vector.quantize_mx(
-                    out=h_w[:, a, cols].bitcast(FP8X4),
-                    scales=h_s[:, a, cols],
-                    in_=h_bf[:, a, cols, :].rearrange("p j t -> p (j t)"),
-                )
+                    if unquantised:
+                        quantize_h(*unquantised.pop())
+                unquantised.append((j0, a))
+
+        en_plane = en_s[:].bitcast(U8)
+        out_tiles = out.rearrange("(g p) j -> p g j", p=P)
 
         def score(j0, width):
-            cols = slice(j0, j0 + width)
-            groups = PASS // width
-            for g0 in range(0, N // P, groups):
-                bank = psum_s.tile([P, groups, width], F32, name="bank_s")
-                for g in range(groups):
+            tiles = BANK // width
+            for g0 in range(0, N // P, tiles):
+                bank = take_bank([P, tiles, width])
+                for g in range(tiles):
                     n_cols = slice((g0 + g) * P, (g0 + g + 1) * P)
                     for a in range(R_PASSES):
                         nc.tensor.matmul_mx(
                             out=bank[:, g, :],
                             lhsT=en_w[:, a, n_cols].bitcast(FP8X4),
-                            lhsT_scale=en_bytes[EN_ROW:P, a, n_cols],
-                            rhs=h_w[:, a, cols].bitcast(FP8X4),
-                            rhs_scale=h_s[:, a, cols],
+                            lhsT_scale=en_plane[EN_ROW:P, a, n_cols],
+                            rhs=h_w[j0][:, a, :].bitcast(FP8X4),
+                            rhs_scale=h_s[j0][:, a, :],
                             start=(a == 0),
                             stop=(a == R_PASSES - 1),
                         )
-                result = stage.tile([P, groups, width], F32, name="result")
+                result = stage.tile([P, tiles, width], F32, name="result")
                 nc.scalar.activation(result[:], bank[:], SIGMOID)
-                nc.sync.dma_start(out=out_tiles[:, g0 : g0 + groups, cols], in_=result[:])
+                nc.sync.dma_start(out=out_tiles[:, g0 : g0 + tiles, j0 : j0 + width], in_=result[:])
 
-        chunks = [(sum(CHUNKS[:c]), CHUNKS[c]) for c in range(len(CHUNKS))]
+        chunks = [(sum(CHUNKS[:c]), width) for c, width in enumerate(CHUNKS)]
         make_h(*chunks[0])
-        for c in range(len(chunks)):
+        for c, chunk in enumerate(chunks):
             if c + 1 < len(chunks):
                 make_h(*chunks[c + 1])
-            score(*chunks[c])
+            else:
+                quantize_h(*unquantised.pop())
+            score(*chunk)

@@ -63,11 +63,6 @@ def tile_list_kg_mul_sig_kernel(
         nc.vector.memset(tab_s[:], 0)
         nc.vector.memset(tab2_s[:], 0)
 
-        warm_in = keep.tile([P, 1], F32, name="warm_in")
-        warm_out = keep.tile([P, 1], F32, name="warm_out")
-        nc.vector.memset(warm_in[:], 0.0)
-        nc.scalar.activation(warm_out[:], warm_in[:], SIGMOID)
-
         for q in range(P // QUADRANT):
             rows = wa_scales[0, PACK * q : PACK * (q + 1), :].bitcast(I32)
             nc.sync.dma_start(

@@ -27,8 +27,8 @@ BANK = 512
 BANKS = 8
 HA_BANKS = 4
 CHUNKS = [128, 256, 256, 256, 128]
-TAB_FIRST = 768
-TAB_ROW, TAB2_ROW, WA_ROW, EN_ROW = 0, 4, 0, 8
+SPREAD_ROW, SPREAD_STEP = 4, 8
+TAB_ROW, TAB2_ROW, WA_ROW, EN_ROW = 0, 0, 0, 8
 STORES = J * N // (P * BANK)
 
 
@@ -48,79 +48,83 @@ def tile_list_kg_mul_sig_kernel(
     nc = tc.nc
     with ExitStack() as ctx:
         keep = ctx.enter_context(tc.tile_pool(name="keep", bufs=1))
-        reuse = ctx.enter_context(tc.tile_pool(name="reuse", bufs=1))
         stage = ctx.enter_context(tc.tile_pool(name="stage", bufs=STORES))
         psum = ctx.enter_context(tc.psum_pool(name="psum", bufs=1))
 
         list_a = keep.tile([P, J // LIST_GROUP], U16, name="list_a")
         list_b = keep.tile([P, J // LIST_GROUP], U16, name="list_b")
-        tab_s = keep.tile([P, 1, T // 4], I32, name="tab_s", align_bytes=64)
-        tab2_s = reuse.tile([P, 1, T // 4], I32, name="tab2_s", tag="tab2_s_en_s", align_bytes=64)
-        wa_raw_w = reuse.tile([P, R], I32, name="wa_raw_w", tag="wa_w_tab2_w", align_bytes=64)
-        wa_raw_s = reuse.tile([P, R // 4], I32, name="wa_raw_s", tag="wa_s_wb", align_bytes=64)
-        tab_w = reuse.tile([P, T], I32, name="tab_w", tag="tab_w_en_w", align_bytes=64)
+        tab_s = keep.tile([P, T // 4], I32, name="tab_s", align_bytes=64)
+        tab2_s = keep.tile([P, T // 4], I32, name="tab2_s", align_bytes=64)
+        wa_raw_s = keep.tile([P, R // 4], I32, name="wa_raw_s", align_bytes=64)
+        wa_raw_w = keep.tile([P, R], I32, name="wa_raw_w", align_bytes=64)
+        tab_w = keep.tile([P, T], I32, name="tab_w", align_bytes=64)
+        tab2_w = keep.tile([P, T], I32, name="tab2_w", align_bytes=64)
+        planes_a = keep.tile([P, (J + R) // 4], I32, name="planes_a", align_bytes=64)
+        plane_b = keep.tile([P, J // 4], I32, name="plane_b", align_bytes=64)
+        en_s = keep.tile([P, R_PASSES, N // 4], I32, name="en_s", align_bytes=64)
+        en_w = keep.tile([P, R_PASSES, N], I32, name="en_w", align_bytes=64)
+        passes = [slice(a * PASS, (a + 1) * PASS) for a in range(R_PASSES)]
+        wb_raw = [keep.tile([P, PACK, PASS], F32, name="wb_raw%d" % a, align_bytes=64) for a in range(R_PASSES)]
 
-        nc.vector.memset(tab_s[:], 0)
-        nc.vector.memset(tab2_s[:], 0)
+        for tile in (tab_s, wa_raw_s, tab2_s, planes_a, plane_b, en_s):
+            nc.vector.memset(tile[:], 0)
 
-        for q in range(P // QUADRANT):
-            rows = wa_scales[0, PACK * q : PACK * (q + 1), :].bitcast(I32)
-            nc.sync.dma_start(
-                out=wa_raw_s[QUADRANT * q : QUADRANT * (q + 1), :],
-                in_=rows.unsqueeze(0).to_broadcast([QUADRANT // PACK, PACK, R // 4]),
-            )
+        spread = slice(SPREAD_ROW, P, SPREAD_STEP)
         nc.sync.dma_start(list_a[:], offs)
         nc.sync.dma_start(list_b[:], offs2)
         nc.sync.dma_start(out=wa_raw_w[:], in_=as_words(wa_words[0]))
-        nc.sync.dma_start(out=tab_w[:, :TAB_FIRST], in_=as_words(tab_words[0])[:, :TAB_FIRST])
-        load_scale_rows(nc, tab_s, TAB_ROW, tab_scales)
-        load_scale_rows(nc, tab2_s, TAB2_ROW, tab2_scales)
-        nc.sync.dma_start(out=tab_w[:, TAB_FIRST:], in_=as_words(tab_words[0])[:, TAB_FIRST:])
+        nc.sync.dma_start(out=tab_s[spread, :], in_=tab_scales[0].bitcast(I32))
+        nc.sync.dma_start(out=wa_raw_s[spread, :], in_=wa_scales[0].bitcast(I32))
+        nc.sync.dma_start(out=tab2_s[spread, :], in_=tab2_scales[0].bitcast(I32))
+        nc.sync.dma_start(out=tab_w[:], in_=as_words(tab_words[0]))
+        wb_rows = wb.rearrange("(p i) r -> p i r", i=PACK)
+        nc.sync.dma_start(out=wb_raw[0][:], in_=wb_rows[:, :, passes[0]])
 
-        wa_w = keep.tile([P, R], I32, name="wa_w", align_bytes=64)
-        wa_s = keep.tile([P, R], U8, name="wa_s", align_bytes=64)
-        passes = [slice(a * PASS, (a + 1) * PASS) for a in range(R_PASSES)]
+        def move_scale_rows(plane, spread_rows):
+            for r in range(PACK):
+                nc.sync.dma_start(
+                    out=plane[r:P:QUADRANT, :],
+                    in_=spread_rows[SPREAD_ROW + SPREAD_STEP * r : P : QUADRANT, :].bitcast(I32),
+                )
+
+        picked_a = keep.tile([P, J], U8, name="picked_a", align_bytes=64)
+        picked_b = keep.tile([P, J], U8, name="picked_b", align_bytes=64)
+        staged_a = keep.tile([P, J + R], U8, name="staged_a", align_bytes=64)
+        nc.vector.tensor_copy(picked_a[:], tab_s[:].bitcast(U8).indirect(list_a[:]))
         for cols in passes:
             nc.vector.tensor_copy(
-                out=wa_s[:, cols].rearrange("p (t m) -> p t m", t=PACK),
+                out=staged_a[:, J:][:, cols].rearrange("p (t m) -> p t m", t=PACK),
                 in_=wa_raw_s[:].bitcast(U8)[:, cols].rearrange("p (m t) -> p t m", t=PACK),
             )
-        wb_raw = reuse.tile([P, R_PASSES, PACK, PASS], F32, name="wb_raw", tag="wa_s_wb", align_bytes=64)
-        wb_rows = wb.rearrange("(p i) r -> p i r", i=PACK)
-        for a, cols in enumerate(passes):
-            nc.sync.dma_start(out=wb_raw[:, a], in_=wb_rows[:, :, cols])
+        nc.vector.tensor_copy(staged_a[:, :J].bitcast(I32), picked_a[:].bitcast(I32))
+        move_scale_rows(planes_a, staged_a)
+        nc.sync.dma_start(out=wb_raw[1][:], in_=wb_rows[:, :, passes[1]])
+        nc.sync.dma_start(out=tab2_w[:], in_=as_words(tab2_words[0]))
+        nc.vector.tensor_copy(picked_b[:], tab2_s[:].bitcast(U8).indirect(list_b[:]))
+        move_scale_rows(plane_b, picked_b)
+        load_scale_rows(nc, en_s, EN_ROW, en_scales)
+        en_view = en_words.rearrange("a p n i -> p a (n i)").bitcast(I32)
+        for n0 in range(0, N, N // 2):
+            nc.sync.dma_start(out=en_w[:, :, n0 : n0 + N // 2], in_=en_view[:, :, n0 : n0 + N // 2])
+        va_s, wa_s = planes_a[:].bitcast(U8)[:, :J], planes_a[:].bitcast(U8)[:, J:]
+        vb_s = plane_b[:].bitcast(U8)
+
+        wa_w = keep.tile([P, R], I32, name="wa_w", align_bytes=64)
         for cols in passes:
             nc.vector.tensor_copy(
                 out=wa_w[:, cols].rearrange("p (t g u) -> p g t u", t=PACK, u=4),
                 in_=wa_raw_w[:, cols].rearrange("p (g u t) -> p g t u", t=PACK, u=4),
             )
-        tab2_w = reuse.tile([P, T], I32, name="tab2_w", tag="wa_w_tab2_w", align_bytes=64)
-        nc.sync.dma_start(out=tab2_w[:], in_=as_words(tab2_words[0]))
 
         va_w = [keep.tile([P, HALF], U32, name="va_w%d" % half, align_bytes=64) for half in range(2)]
         vb_w = [keep.tile([P, HALF], U32, name="vb_w%d" % half, align_bytes=64) for half in range(2)]
-        va_s = keep.tile([P, J], U8, name="va_s", align_bytes=64)
-        vb_s = keep.tile([P, J], U8, name="vb_s", align_bytes=64)
-
-        def gather_scales(picked, plane, offsets):
-            window = plane[:].rearrange("p a t -> p (a t)").bitcast(U8)
-            nc.vector.tensor_copy(picked[:], window.indirect(offsets[:]))
 
         def gather_words(picked, table, offsets):
             for half in range(2):
                 entries = offsets[:, half * HALF // LIST_GROUP : (half + 1) * HALF // LIST_GROUP]
                 nc.vector.tensor_copy(picked[half][:], table[:].bitcast(U32).indirect(entries))
 
-        gather_scales(va_s, tab_s, list_a)
-        gather_scales(vb_s, tab2_s, list_b)
-        en_s = reuse.tile([P, R_PASSES, N // 4], I32, name="en_s", tag="tab2_s_en_s", align_bytes=64)
-        nc.vector.memset(en_s[:], 0)
-        load_scale_rows(nc, en_s, EN_ROW, en_scales)
         gather_words(va_w, tab_w, list_a)
-        en_w = reuse.tile([P, R_PASSES, N], I32, name="en_w", tag="tab_w_en_w", align_bytes=64)
-        en_view = en_words.rearrange("a p n i -> p a (n i)").bitcast(I32)
-        for n0 in range(0, N, N // 2):
-            nc.sync.dma_start(out=en_w[:, :, n0 : n0 + N // 2], in_=en_view[:, :, n0 : n0 + N // 2])
 
         wb_w = keep.tile([P, R], U32, name="wb_w", align_bytes=64)
         wb_s = keep.tile([P, R], U8, name="wb_s", align_bytes=64)
@@ -128,7 +132,7 @@ def tile_list_kg_mul_sig_kernel(
             wb_bf = keep.tile([P, PASS * PACK], BF16, name="wb_bf%d" % a, align_bytes=64)
             nc.vector.tensor_copy(
                 out=wb_bf[:].rearrange("p (t m i) -> p m t i", t=PACK, i=PACK),
-                in_=wb_raw[:, a].rearrange("p i (m t) -> p m t i", t=PACK),
+                in_=wb_raw[a][:].rearrange("p i (m t) -> p m t i", t=PACK),
             )
             nc.vector.quantize_mx(out=wb_w[:, cols].bitcast(FP8X4), scales=wb_s[:, cols], in_=wb_bf[:])
         gather_words(vb_w, tab2_w, list_b)

@@ -25,21 +25,15 @@ HALF = J // 2
 PIECE = P
 BANK = 512
 BANKS = 8
-HA_BANKS = 4
-CHUNKS = [128, 256, 256, 256, 128]
+LEAD = 5
+CHUNKS = [1, 1, 2, 2, 2]
+PIECES = J // PIECE
 SPREAD_ROW, SPREAD_STEP = 4, 8
-TAB_ROW, TAB2_ROW, WA_ROW, EN_ROW = 0, 0, 0, 8
-STORES = J * N // (P * BANK)
+VECTOR_PIECES = range(2)
 
 
 def as_words(codes):
     return codes.rearrange("p n i -> p (n i)").bitcast(I32)
-
-
-def load_scale_rows(nc, plane, first_row, scales):
-    by_row = scales.rearrange("a (q r) n -> r q a n", r=PACK)
-    for r in range(PACK):
-        nc.sync.dma_start(out=plane[first_row + r : P : QUADRANT], in_=by_row[r].bitcast(I32))
 
 
 def tile_list_kg_mul_sig_kernel(
@@ -48,7 +42,6 @@ def tile_list_kg_mul_sig_kernel(
     nc = tc.nc
     with ExitStack() as ctx:
         keep = ctx.enter_context(tc.tile_pool(name="keep", bufs=1))
-        stage = ctx.enter_context(tc.tile_pool(name="stage", bufs=STORES))
         psum = ctx.enter_context(tc.psum_pool(name="psum", bufs=1))
 
         list_a = keep.tile([P, J // LIST_GROUP], U16, name="list_a")
@@ -59,26 +52,15 @@ def tile_list_kg_mul_sig_kernel(
         wa_raw_w = keep.tile([P, R], I32, name="wa_raw_w", align_bytes=64)
         tab_w = keep.tile([P, T], I32, name="tab_w", align_bytes=64)
         tab2_w = keep.tile([P, T], I32, name="tab2_w", align_bytes=64)
-        planes_a = keep.tile([P, (J + R) // 4], I32, name="planes_a", align_bytes=64)
+        staged_a = keep.tile([P, J + R + R_PASSES * N], U8, name="staged_a", align_bytes=64)
+        planes_a = keep.tile([P, (J + R + R_PASSES * N) // 4], I32, name="planes_a", align_bytes=64)
         plane_b = keep.tile([P, J // 4], I32, name="plane_b", align_bytes=64)
-        en_s = keep.tile([P, R_PASSES, N // 4], I32, name="en_s", align_bytes=64)
         en_w = keep.tile([P, R_PASSES, N], I32, name="en_w", align_bytes=64)
         passes = [slice(a * PASS, (a + 1) * PASS) for a in range(R_PASSES)]
         wb_raw = [keep.tile([P, PACK, PASS], F32, name="wb_raw%d" % a, align_bytes=64) for a in range(R_PASSES)]
 
-        for tile in (tab_s, wa_raw_s, tab2_s, planes_a, plane_b, en_s):
+        for tile in (tab2_s, tab_s, wa_raw_s, plane_b, planes_a):
             nc.vector.memset(tile[:], 0)
-
-        spread = slice(SPREAD_ROW, P, SPREAD_STEP)
-        nc.sync.dma_start(list_a[:], offs)
-        nc.sync.dma_start(list_b[:], offs2)
-        nc.sync.dma_start(out=wa_raw_w[:], in_=as_words(wa_words[0]))
-        nc.sync.dma_start(out=tab_s[spread, :], in_=tab_scales[0].bitcast(I32))
-        nc.sync.dma_start(out=wa_raw_s[spread, :], in_=wa_scales[0].bitcast(I32))
-        nc.sync.dma_start(out=tab2_s[spread, :], in_=tab2_scales[0].bitcast(I32))
-        nc.sync.dma_start(out=tab_w[:], in_=as_words(tab_words[0]))
-        wb_rows = wb.rearrange("(p i) r -> p i r", i=PACK)
-        nc.sync.dma_start(out=wb_raw[0][:], in_=wb_rows[:, :, passes[0]])
 
         def move_scale_rows(plane, spread_rows):
             for r in range(PACK):
@@ -87,26 +69,64 @@ def tile_list_kg_mul_sig_kernel(
                     in_=spread_rows[SPREAD_ROW + SPREAD_STEP * r : P : QUADRANT, :].bitcast(I32),
                 )
 
+        spread = slice(SPREAD_ROW, P, SPREAD_STEP)
+        wb_rows = wb.rearrange("(p i) r -> p i r", i=PACK)
+        nc.sync.dma_start(list_b[:], offs2)
+        nc.sync.dma_start(list_a[:], offs)
+        nc.sync.dma_start(out=wb_raw[0][:, :2], in_=wb_rows[:, :2, passes[0]])
+        nc.sync.dma_start(out=tab2_s[spread, :], in_=tab2_scales[0].bitcast(I32))
+        nc.sync.dma_start(out=wb_raw[0][:, 2:], in_=wb_rows[:, 2:, passes[0]])
+        nc.sync.dma_start(out=tab_s[spread, :], in_=tab_scales[0].bitcast(I32))
+        nc.sync.dma_start(out=wa_raw_s[spread, :], in_=wa_scales[0].bitcast(I32))
+        nc.sync.dma_start(out=tab2_w[:], in_=as_words(tab2_words[0]))
+        nc.sync.dma_start(
+            out=staged_a[spread, J + R :].bitcast(I32).rearrange("q (a n) -> q a n", a=R_PASSES),
+            in_=en_scales.rearrange("a q n -> q a n").bitcast(I32),
+        )
+
         picked_a = keep.tile([P, J], U8, name="picked_a", align_bytes=64)
         picked_b = keep.tile([P, J], U8, name="picked_b", align_bytes=64)
-        staged_a = keep.tile([P, J + R], U8, name="staged_a", align_bytes=64)
+        nc.vector.tensor_copy(picked_b[:], tab2_s[:].bitcast(U8).indirect(list_b[:]))
+        move_scale_rows(plane_b, picked_b)
+        nc.sync.dma_start(out=wb_raw[1][:], in_=wb_rows[:, :, passes[1]])
+        nc.sync.dma_start(out=wa_raw_w[:], in_=as_words(wa_words[0]))
+        nc.sync.dma_start(out=tab_w[:], in_=as_words(tab_words[0]))
+
+        va_w = [keep.tile([P, HALF], U32, name="va_w%d" % half, align_bytes=64) for half in range(2)]
+        vb_w = [keep.tile([P, HALF], U32, name="vb_w%d" % half, align_bytes=64) for half in range(2)]
+
+        def gather_words(picked, table, offsets, half):
+            entries = offsets[:, half * HALF // LIST_GROUP : (half + 1) * HALF // LIST_GROUP]
+            nc.vector.tensor_copy(picked[half][:], table[:].bitcast(U32).indirect(entries))
+
+        for half in range(2):
+            gather_words(vb_w, tab2_w, list_b, half)
+
+        wb_w = keep.tile([P, R], U32, name="wb_w", align_bytes=64)
+        wb_s = keep.tile([P, R], U8, name="wb_s", align_bytes=64)
+        for a, cols in enumerate(passes):
+            wb_bf = keep.tile([P, PASS * PACK], BF16, name="wb_bf%d" % a, align_bytes=64)
+            copy = nc.scalar.copy if a == 0 else nc.vector.tensor_copy
+            copy(
+                out=wb_bf[:].rearrange("p (t m i) -> p m t i", t=PACK, i=PACK),
+                in_=wb_raw[a][:].rearrange("p i (m t) -> p m t i", t=PACK),
+            )
+            nc.vector.quantize_mx(out=wb_w[:, cols].bitcast(FP8X4), scales=wb_s[:, cols], in_=wb_bf[:])
+
         nc.vector.tensor_copy(picked_a[:], tab_s[:].bitcast(U8).indirect(list_a[:]))
         for cols in passes:
             nc.vector.tensor_copy(
-                out=staged_a[:, J:][:, cols].rearrange("p (t m) -> p t m", t=PACK),
+                out=staged_a[:, J : J + R][:, cols].rearrange("p (t m) -> p t m", t=PACK),
                 in_=wa_raw_s[:].bitcast(U8)[:, cols].rearrange("p (m t) -> p t m", t=PACK),
             )
         nc.vector.tensor_copy(staged_a[:, :J].bitcast(I32), picked_a[:].bitcast(I32))
         move_scale_rows(planes_a, staged_a)
-        nc.sync.dma_start(out=wb_raw[1][:], in_=wb_rows[:, :, passes[1]])
-        nc.sync.dma_start(out=tab2_w[:], in_=as_words(tab2_words[0]))
-        nc.vector.tensor_copy(picked_b[:], tab2_s[:].bitcast(U8).indirect(list_b[:]))
-        move_scale_rows(plane_b, picked_b)
-        load_scale_rows(nc, en_s, EN_ROW, en_scales)
         en_view = en_words.rearrange("a p n i -> p a (n i)").bitcast(I32)
         for n0 in range(0, N, N // 2):
             nc.sync.dma_start(out=en_w[:, :, n0 : n0 + N // 2], in_=en_view[:, :, n0 : n0 + N // 2])
-        va_s, wa_s = planes_a[:].bitcast(U8)[:, :J], planes_a[:].bitcast(U8)[:, J:]
+        plane_bytes = planes_a[:].bitcast(U8)
+        va_s, wa_s = plane_bytes[:, :J], plane_bytes[:, J : J + R]
+        en_plane = plane_bytes[:, J + R :].rearrange("p (a n) -> p a n", a=R_PASSES)
         vb_s = plane_b[:].bitcast(U8)
 
         wa_w = keep.tile([P, R], I32, name="wa_w", align_bytes=64)
@@ -115,27 +135,6 @@ def tile_list_kg_mul_sig_kernel(
                 out=wa_w[:, cols].rearrange("p (t g u) -> p g t u", t=PACK, u=4),
                 in_=wa_raw_w[:, cols].rearrange("p (g u t) -> p g t u", t=PACK, u=4),
             )
-
-        va_w = [keep.tile([P, HALF], U32, name="va_w%d" % half, align_bytes=64) for half in range(2)]
-        vb_w = [keep.tile([P, HALF], U32, name="vb_w%d" % half, align_bytes=64) for half in range(2)]
-
-        def gather_words(picked, table, offsets):
-            for half in range(2):
-                entries = offsets[:, half * HALF // LIST_GROUP : (half + 1) * HALF // LIST_GROUP]
-                nc.vector.tensor_copy(picked[half][:], table[:].bitcast(U32).indirect(entries))
-
-        gather_words(va_w, tab_w, list_a)
-
-        wb_w = keep.tile([P, R], U32, name="wb_w", align_bytes=64)
-        wb_s = keep.tile([P, R], U8, name="wb_s", align_bytes=64)
-        for a, cols in enumerate(passes):
-            wb_bf = keep.tile([P, PASS * PACK], BF16, name="wb_bf%d" % a, align_bytes=64)
-            nc.vector.tensor_copy(
-                out=wb_bf[:].rearrange("p (t m i) -> p m t i", t=PACK, i=PACK),
-                in_=wb_raw[a][:].rearrange("p i (m t) -> p m t i", t=PACK),
-            )
-            nc.vector.quantize_mx(out=wb_w[:, cols].bitcast(FP8X4), scales=wb_s[:, cols], in_=wb_bf[:])
-        gather_words(vb_w, tab2_w, list_b)
 
         def project(bank, w_words, w_scales, w_row, v_words, v_scales, v_row, a, j0):
             for t in range(PACK):
@@ -150,76 +149,77 @@ def tile_list_kg_mul_sig_kernel(
                     stop=True,
                 )
 
-        ha = keep.tile([P, J // PIECE, R_PASSES, PIECE, PACK], F32, name="ha", align_bytes=64)
-        for piece in range(J // PIECE):
-            for a in range(R_PASSES):
-                tag = "bank%d" % ((piece * R_PASSES + a) % HA_BANKS)
-                bank = psum.tile([P, PACK, PIECE], F32, name="ha_bank", tag=tag)
-                project(bank, wa_w, wa_s, WA_ROW, va_w, va_s, TAB_ROW, a, piece * PIECE)
-                nc.scalar.copy(out=ha[:, piece, a], in_=bank[:].rearrange("p t j -> p j t"))
+        def take_bank(number, shape):
+            return psum.tile(shape, F32, name="bank", tag="bank%d" % (number % BANKS))
 
-        taken = []
+        hb = keep.tile([P, J // PIECE, R_PASSES, PIECE, PACK], F32, name="hb", align_bytes=64)
+        for a in range(R_PASSES):
+            for piece in range(J // PIECE):
+                bank = take_bank(piece, [P, PACK, PIECE])
+                project(bank, wb_w, wb_s, 0, vb_w, vb_s, 0, a, piece * PIECE)
+                if a == 1 and piece in VECTOR_PIECES:
+                    nc.vector.tensor_copy(out=hb[:, piece, a], in_=bank[:].rearrange("p t j -> p j t"))
+                else:
+                    nc.scalar.copy(out=hb[:, piece, a], in_=bank[:].rearrange("p t j -> p j t"))
+        for half in range(2):
+            gather_words(va_w, tab_w, list_a, half)
 
-        def take_bank(shape):
-            taken.append(shape)
-            return psum.tile(shape, F32, name="bank", tag="bank%d" % ((HA_BANKS + len(taken) - 1) % BANKS))
-
-        h_bf, h_w, h_s = {}, {}, {}
+        firsts = [sum(CHUNKS[:c]) for c in range(len(CHUNKS))]
+        h_w, h_s = {}, {}
+        for first, count in zip(firsts, CHUNKS):
+            h_w[first] = keep.tile([P, R_PASSES, count * PIECE], U32, name="h_w%d" % first, align_bytes=64)
+            h_s[first] = keep.tile([P, R_PASSES, count * PIECE], U8, name="h_s%d" % first, align_bytes=64)
         unquantised = []
 
-        def quantize_h(j0, a):
+        def quantize_h(h_bf, piece, a):
+            first = max(f for f in firsts if f <= piece)
+            cols = slice((piece - first) * PIECE, (piece - first + 1) * PIECE)
             nc.vector.quantize_mx(
-                out=h_w[j0][:, a].bitcast(FP8X4),
-                scales=h_s[j0][:, a],
-                in_=h_bf[j0][:, a].rearrange("p j t -> p (j t)"),
+                out=h_w[first][:, a, cols].bitcast(FP8X4),
+                scales=h_s[first][:, a, cols],
+                in_=h_bf[:].rearrange("p j t -> p (j t)"),
             )
 
-        def make_h(j0, width):
-            h_bf[j0] = keep.tile([P, R_PASSES, width, PACK], BF16, name="h_bf%d" % j0, align_bytes=64)
-            h_w[j0] = keep.tile([P, R_PASSES, width], U32, name="h_w%d" % j0, align_bytes=64)
-            h_s[j0] = keep.tile([P, R_PASSES, width], U8, name="h_s%d" % j0, align_bytes=64)
+        def make_h(piece):
             for a in range(R_PASSES):
-                for j1 in range(0, width, PIECE):
-                    bank = take_bank([P, PACK, PIECE])
-                    project(bank, wb_w, wb_s, 0, vb_w, vb_s, TAB2_ROW, a, j0 + j1)
-                    nc.vector.tensor_tensor(
-                        h_bf[j0][:, a, j1 : j1 + PIECE, :],
-                        bank[:].rearrange("p t j -> p j t"),
-                        ha[:, (j0 + j1) // PIECE, a],
-                        MULT,
-                    )
-                    if unquantised:
-                        quantize_h(*unquantised.pop())
-                unquantised.append((j0, a))
+                tag = "h_bf%d_%d" % (piece, a)
+                h_bf = keep.tile([P, PIECE, PACK], BF16, name=tag, tag=tag, align_bytes=64)
+                bank = take_bank(R_PASSES * piece + a, [P, PACK, PIECE])
+                project(bank, wa_w, wa_s, 0, va_w, va_s, 0, a, piece * PIECE)
+                nc.vector.tensor_tensor(h_bf[:], bank[:].rearrange("p t j -> p j t"), hb[:, piece, a], MULT)
+                if unquantised:
+                    quantize_h(*unquantised.pop())
+                unquantised.append((h_bf, piece, a))
+            if piece == PIECES - 1:
+                quantize_h(*unquantised.pop())
 
-        en_plane = en_s[:].bitcast(U8)
         out_tiles = out.rearrange("(g p) j -> p g j", p=P)
 
-        def score(j0, width):
+        def score(first, count):
+            width = count * PIECE
             tiles = BANK // width
             for g0 in range(0, N // P, tiles):
-                bank = take_bank([P, tiles, width])
+                bank = take_bank(R_PASSES * (first + 1) + g0 // tiles, [P, tiles, width])
                 for g in range(tiles):
                     n_cols = slice((g0 + g) * P, (g0 + g + 1) * P)
                     for a in range(R_PASSES):
                         nc.tensor.matmul_mx(
                             out=bank[:, g, :],
                             lhsT=en_w[:, a, n_cols].bitcast(FP8X4),
-                            lhsT_scale=en_plane[EN_ROW:P, a, n_cols],
-                            rhs=h_w[j0][:, a, :].bitcast(FP8X4),
-                            rhs_scale=h_s[j0][:, a, :],
+                            lhsT_scale=en_plane[:, a, n_cols],
+                            rhs=h_w[first][:, a, :].bitcast(FP8X4),
+                            rhs_scale=h_s[first][:, a, :],
                             start=(a == 0),
                             stop=(a == R_PASSES - 1),
                         )
-                result = stage.tile([P, tiles, width], F32, name="result")
+                result = keep.tile([P, tiles, width], F32, name="result%d_%d" % (first, g0))
                 nc.scalar.activation(result[:], bank[:], SIGMOID)
-                nc.sync.dma_start(out=out_tiles[:, g0 : g0 + tiles, j0 : j0 + width], in_=result[:])
+                queries = slice(first * PIECE, first * PIECE + width)
+                nc.sync.dma_start(out=out_tiles[:, g0 : g0 + tiles, queries], in_=result[:])
 
-        chunks = [(sum(CHUNKS[:c]), width) for c, width in enumerate(CHUNKS)]
-        make_h(*chunks[0])
-        for c, chunk in enumerate(chunks):
-            if c + 1 < len(chunks):
-                make_h(*chunks[c + 1])
-            else:
-                quantize_h(*unquantised.pop())
-            score(*chunk)
+        for piece in range(LEAD):
+            make_h(piece)
+        for c, (first, count) in enumerate(zip(firsts, CHUNKS)):
+            score(first, count)
+            if c + LEAD < PIECES:
+                make_h(c + LEAD)

@@ -28,7 +28,7 @@ BANKS = 8
 LEAD = 5
 CHUNKS = [1, 1, 2, 2, 2]
 PIECES = J // PIECE
-SPREAD_ROW, SPREAD_STEP = 4, 8
+SPREAD_ROW, SPREAD_STEP, SCALE_ROWS = 32, 4, 16
 VECTOR_PIECES = range(2)
 
 
@@ -62,18 +62,22 @@ def tile_list_kg_mul_sig_kernel(
         for tile in (tab2_s, tab_s, wa_raw_s, plane_b, planes_a):
             nc.vector.memset(tile[:], 0)
 
+        warm = keep.tile([P, 2], F32, name="warm")
+        nc.gpsimd.memset(warm[:, :1], 0.0)
+        nc.scalar.activation(warm[:, 1:], warm[:, :1], SIGMOID)
+
         def move_scale_rows(plane, spread_rows):
             for r in range(PACK):
                 nc.sync.dma_start(
                     out=plane[r:P:QUADRANT, :],
-                    in_=spread_rows[SPREAD_ROW + SPREAD_STEP * r : P : QUADRANT, :].bitcast(I32),
+                    in_=spread_rows[SPREAD_ROW + SPREAD_STEP * r : SPREAD_ROW + SPREAD_STEP * SCALE_ROWS : SPREAD_STEP * PACK, :].bitcast(I32),
                 )
 
-        spread = slice(SPREAD_ROW, P, SPREAD_STEP)
+        spread = slice(SPREAD_ROW, SPREAD_ROW + SPREAD_STEP * SCALE_ROWS, SPREAD_STEP)
         wb_rows = wb.rearrange("(p i) r -> p i r", i=PACK)
+        nc.sync.dma_start(out=wb_raw[0][:, :2], in_=wb_rows[:, :2, passes[0]])
         nc.sync.dma_start(list_b[:], offs2)
         nc.sync.dma_start(list_a[:], offs)
-        nc.sync.dma_start(out=wb_raw[0][:, :2], in_=wb_rows[:, :2, passes[0]])
         nc.sync.dma_start(out=tab2_s[spread, :], in_=tab2_scales[0].bitcast(I32))
         nc.sync.dma_start(out=wb_raw[0][:, 2:], in_=wb_rows[:, 2:, passes[0]])
         nc.sync.dma_start(out=tab_s[spread, :], in_=tab_scales[0].bitcast(I32))
@@ -155,7 +159,7 @@ def tile_list_kg_mul_sig_kernel(
         hb = keep.tile([P, J // PIECE, R_PASSES, PIECE, PACK], F32, name="hb", align_bytes=64)
         for a in range(R_PASSES):
             for piece in range(J // PIECE):
-                bank = take_bank(piece, [P, PACK, PIECE])
+                bank = take_bank(piece if a == 0 else piece % (BANKS // 2), [P, PACK, PIECE])
                 project(bank, wb_w, wb_s, 0, vb_w, vb_s, 0, a, piece * PIECE)
                 if a == 1 and piece in VECTOR_PIECES:
                     nc.vector.tensor_copy(out=hb[:, piece, a], in_=bank[:].rearrange("p t j -> p j t"))
@@ -184,7 +188,7 @@ def tile_list_kg_mul_sig_kernel(
             for a in range(R_PASSES):
                 tag = "h_bf%d_%d" % (piece, a)
                 h_bf = keep.tile([P, PIECE, PACK], BF16, name=tag, tag=tag, align_bytes=64)
-                bank = take_bank(R_PASSES * piece + a, [P, PACK, PIECE])
+                bank = take_bank(R_PASSES * (piece + 2) + a, [P, PACK, PIECE])
                 project(bank, wa_w, wa_s, 0, va_w, va_s, 0, a, piece * PIECE)
                 nc.vector.tensor_tensor(h_bf[:], bank[:].rearrange("p t j -> p j t"), hb[:, piece, a], MULT)
                 if unquantised:
@@ -199,7 +203,7 @@ def tile_list_kg_mul_sig_kernel(
             width = count * PIECE
             tiles = BANK // width
             for g0 in range(0, N // P, tiles):
-                bank = take_bank(R_PASSES * (first + 1) + g0 // tiles, [P, tiles, width])
+                bank = take_bank(R_PASSES * (first + 3) + g0 // tiles, [P, tiles, width])
                 for g in range(tiles):
                     n_cols = slice((g0 + g) * P, (g0 + g + 1) * P)
                     for a in range(R_PASSES):

@@ -29,7 +29,7 @@ LEAD = 5
 CHUNKS = [1, 1, 2, 2, 2]
 PIECES = J // PIECE
 SPREAD_ROW, SPREAD_STEP, SCALE_ROWS = 32, 4, 16
-VECTOR_PIECES = range(2)
+VECTOR_PIECES = range(1)
 
 
 def as_words(codes):
@@ -169,41 +169,49 @@ def tile_list_kg_mul_sig_kernel(
             gather_words(va_w, tab_w, list_a, half)
 
         firsts = [sum(CHUNKS[:c]) for c in range(len(CHUNKS))]
-        h_w, h_s = {}, {}
+        h_bf, h_w, h_s = {}, {}, {}
         for first, count in zip(firsts, CHUNKS):
+            h_bf[first] = keep.tile([P, R_PASSES * count, PIECE, PACK], BF16, name="h_bf%d" % first, align_bytes=64)
             h_w[first] = keep.tile([P, R_PASSES, count * PIECE], U32, name="h_w%d" % first, align_bytes=64)
             h_s[first] = keep.tile([P, R_PASSES, count * PIECE], U8, name="h_s%d" % first, align_bytes=64)
-        unquantised = []
+        steps = [
+            (first, a * count + j, first + j, a)
+            for first, count in zip(firsts, CHUNKS)
+            for a in range(R_PASSES)
+            for j in range(count)
+        ]
 
-        def quantize_h(h_bf, piece, a):
-            first = max(f for f in firsts if f <= piece)
-            cols = slice((piece - first) * PIECE, (piece - first + 1) * PIECE)
+        def quantize_h(first, slot):
+            cols = slice((slot - 1) * PIECE, (slot + 1) * PIECE)
             nc.vector.quantize_mx(
-                out=h_w[first][:, a, cols].bitcast(FP8X4),
-                scales=h_s[first][:, a, cols],
-                in_=h_bf[:].rearrange("p j t -> p (j t)"),
+                out=h_w[first][:].rearrange("p a j -> p (a j)")[:, cols].bitcast(FP8X4),
+                scales=h_s[first][:].rearrange("p a j -> p (a j)")[:, cols],
+                in_=h_bf[first][:, slot - 1 : slot + 1].rearrange("p s j t -> p (s j t)"),
             )
 
-        def make_h(piece):
-            for a in range(R_PASSES):
-                tag = "h_bf%d_%d" % (piece, a)
-                h_bf = keep.tile([P, PIECE, PACK], BF16, name=tag, tag=tag, align_bytes=64)
-                bank = take_bank(R_PASSES * (piece + 2) + a, [P, PACK, PIECE])
+        def make_h(pair):
+            for step in (2 * pair, 2 * pair + 1):
+                first, slot, piece, a = steps[step]
+                bank = take_bank(step + BANKS // 2, [P, PACK, PIECE])
                 project(bank, wa_w, wa_s, 0, va_w, va_s, 0, a, piece * PIECE)
-                nc.vector.tensor_tensor(h_bf[:], bank[:].rearrange("p t j -> p j t"), hb[:, piece, a], MULT)
-                if unquantised:
-                    quantize_h(*unquantised.pop())
-                unquantised.append((h_bf, piece, a))
-            if piece == PIECES - 1:
-                quantize_h(*unquantised.pop())
+                nc.vector.tensor_tensor(
+                    h_bf[first][:, slot], bank[:].rearrange("p t j -> p j t"), hb[:, piece, a], MULT
+                )
+                if step % 2 == 0 and step > 0:
+                    quantize_h(*steps[step - 1][:2])
+            if pair == PIECES - 1:
+                quantize_h(first, slot)
 
         out_tiles = out.rearrange("(g p) j -> p g j", p=P)
 
         def score(first, count):
             width = count * PIECE
-            tiles = BANK // width
-            for g0 in range(0, N // P, tiles):
-                bank = take_bank(R_PASSES * (first + 3) + g0 // tiles, [P, tiles, width])
+            starts = list(range(0, N // P, BANK // width))
+            if first + count == PIECES:
+                starts.append(N // P - 1)
+            for b, (g0, g1) in enumerate(zip(starts, starts[1:] + [N // P])):
+                tiles = g1 - g0
+                bank = take_bank(R_PASSES * (first + 3) + b, [P, tiles, width])
                 for g in range(tiles):
                     n_cols = slice((g0 + g) * P, (g0 + g + 1) * P)
                     for a in range(R_PASSES):

@@ -20,20 +20,27 @@ PACK = 4
 PASS = P * PACK
 R_PASSES = R // PASS
 QUADRANT = 32
+SCALE_ROWS = P // 8
 LIST_GROUP = 16
 HALF = J // 2
 PIECE = P
+PIECES = J // PIECE
 BANK = 512
 BANKS = 8
-LEAD = 5
+SPREAD_FIRST, SPREAD_STEP = 32, 4
+SPREAD_END = SPREAD_FIRST + SPREAD_STEP * SCALE_ROWS
 CHUNKS = [1, 1, 2, 2, 2]
-PIECES = J // PIECE
-SPREAD_ROW, SPREAD_STEP, SCALE_ROWS = 32, 4, 16
-VECTOR_PIECES = range(1)
+LEAD = BANKS // R_PASSES + 1
 
 
 def as_words(codes):
     return codes.rearrange("p n i -> p (n i)").bitcast(I32)
+
+
+def move_scale_rows(nc, plane, spread_rows):
+    for r in range(PACK):
+        rows = slice(SPREAD_FIRST + SPREAD_STEP * r, SPREAD_END, SPREAD_STEP * PACK)
+        nc.sync.dma_start(out=plane[r:P:QUADRANT, :], in_=spread_rows[rows, :].bitcast(I32))
 
 
 def tile_list_kg_mul_sig_kernel(
@@ -62,24 +69,13 @@ def tile_list_kg_mul_sig_kernel(
         for tile in (tab2_s, tab_s, wa_raw_s, plane_b, planes_a):
             nc.vector.memset(tile[:], 0)
 
-        warm = keep.tile([P, 2], F32, name="warm")
-        nc.gpsimd.memset(warm[:, :1], 0.0)
-        nc.scalar.activation(warm[:, 1:], warm[:, :1], SIGMOID)
-
-        def move_scale_rows(plane, spread_rows):
-            for r in range(PACK):
-                nc.sync.dma_start(
-                    out=plane[r:P:QUADRANT, :],
-                    in_=spread_rows[SPREAD_ROW + SPREAD_STEP * r : SPREAD_ROW + SPREAD_STEP * SCALE_ROWS : SPREAD_STEP * PACK, :].bitcast(I32),
-                )
-
-        spread = slice(SPREAD_ROW, SPREAD_ROW + SPREAD_STEP * SCALE_ROWS, SPREAD_STEP)
+        spread = slice(SPREAD_FIRST, SPREAD_END, SPREAD_STEP)
         wb_rows = wb.rearrange("(p i) r -> p i r", i=PACK)
-        nc.sync.dma_start(out=wb_raw[0][:, :2], in_=wb_rows[:, :2, passes[0]])
+        nc.sync.dma_start(out=wb_raw[0][:, : PACK // 2], in_=wb_rows[:, : PACK // 2, passes[0]])
         nc.sync.dma_start(list_b[:], offs2)
         nc.sync.dma_start(list_a[:], offs)
         nc.sync.dma_start(out=tab2_s[spread, :], in_=tab2_scales[0].bitcast(I32))
-        nc.sync.dma_start(out=wb_raw[0][:, 2:], in_=wb_rows[:, 2:, passes[0]])
+        nc.sync.dma_start(out=wb_raw[0][:, PACK // 2 :], in_=wb_rows[:, PACK // 2 :, passes[0]])
         nc.sync.dma_start(out=tab_s[spread, :], in_=tab_scales[0].bitcast(I32))
         nc.sync.dma_start(out=wa_raw_s[spread, :], in_=wa_scales[0].bitcast(I32))
         nc.sync.dma_start(out=tab2_w[:], in_=as_words(tab2_words[0]))
@@ -91,7 +87,7 @@ def tile_list_kg_mul_sig_kernel(
         picked_a = keep.tile([P, J], U8, name="picked_a", align_bytes=64)
         picked_b = keep.tile([P, J], U8, name="picked_b", align_bytes=64)
         nc.vector.tensor_copy(picked_b[:], tab2_s[:].bitcast(U8).indirect(list_b[:]))
-        move_scale_rows(plane_b, picked_b)
+        move_scale_rows(nc, plane_b, picked_b)
         nc.sync.dma_start(out=wb_raw[1][:], in_=wb_rows[:, :, passes[1]])
         nc.sync.dma_start(out=wa_raw_w[:], in_=as_words(wa_words[0]))
         nc.sync.dma_start(out=tab_w[:], in_=as_words(tab_words[0]))
@@ -99,23 +95,22 @@ def tile_list_kg_mul_sig_kernel(
         va_w = [keep.tile([P, HALF], U32, name="va_w%d" % half, align_bytes=64) for half in range(2)]
         vb_w = [keep.tile([P, HALF], U32, name="vb_w%d" % half, align_bytes=64) for half in range(2)]
 
-        def gather_words(picked, table, offsets, half):
-            entries = offsets[:, half * HALF // LIST_GROUP : (half + 1) * HALF // LIST_GROUP]
-            nc.vector.tensor_copy(picked[half][:], table[:].bitcast(U32).indirect(entries))
+        def gather_words(picked, table, offsets):
+            for half in range(2):
+                entries = offsets[:, half * HALF // LIST_GROUP : (half + 1) * HALF // LIST_GROUP]
+                nc.vector.tensor_copy(picked[half][:], table[:].bitcast(U32).indirect(entries))
 
-        for half in range(2):
-            gather_words(vb_w, tab2_w, list_b, half)
+        gather_words(vb_w, tab2_w, list_b)
 
         wb_w = keep.tile([P, R], U32, name="wb_w", align_bytes=64)
         wb_s = keep.tile([P, R], U8, name="wb_s", align_bytes=64)
-        for a, cols in enumerate(passes):
+        for a, round_copy in enumerate((nc.scalar.copy, nc.vector.tensor_copy)):
             wb_bf = keep.tile([P, PASS * PACK], BF16, name="wb_bf%d" % a, align_bytes=64)
-            copy = nc.scalar.copy if a == 0 else nc.vector.tensor_copy
-            copy(
+            round_copy(
                 out=wb_bf[:].rearrange("p (t m i) -> p m t i", t=PACK, i=PACK),
                 in_=wb_raw[a][:].rearrange("p i (m t) -> p m t i", t=PACK),
             )
-            nc.vector.quantize_mx(out=wb_w[:, cols].bitcast(FP8X4), scales=wb_s[:, cols], in_=wb_bf[:])
+            nc.vector.quantize_mx(out=wb_w[:, passes[a]].bitcast(FP8X4), scales=wb_s[:, passes[a]], in_=wb_bf[:])
 
         nc.vector.tensor_copy(picked_a[:], tab_s[:].bitcast(U8).indirect(list_a[:]))
         for cols in passes:
@@ -124,13 +119,13 @@ def tile_list_kg_mul_sig_kernel(
                 in_=wa_raw_s[:].bitcast(U8)[:, cols].rearrange("p (m t) -> p t m", t=PACK),
             )
         nc.vector.tensor_copy(staged_a[:, :J].bitcast(I32), picked_a[:].bitcast(I32))
-        move_scale_rows(planes_a, staged_a)
+        move_scale_rows(nc, planes_a, staged_a)
         en_view = en_words.rearrange("a p n i -> p a (n i)").bitcast(I32)
         for n0 in range(0, N, N // 2):
             nc.sync.dma_start(out=en_w[:, :, n0 : n0 + N // 2], in_=en_view[:, :, n0 : n0 + N // 2])
         plane_bytes = planes_a[:].bitcast(U8)
         va_s, wa_s = plane_bytes[:, :J], plane_bytes[:, J : J + R]
-        en_plane = plane_bytes[:, J + R :].rearrange("p (a n) -> p a n", a=R_PASSES)
+        en_s = plane_bytes[:, J + R :].rearrange("p (a n) -> p a n", a=R_PASSES)
         vb_s = plane_b[:].bitcast(U8)
 
         wa_w = keep.tile([P, R], I32, name="wa_w", align_bytes=64)
@@ -140,33 +135,32 @@ def tile_list_kg_mul_sig_kernel(
                 in_=wa_raw_w[:, cols].rearrange("p (g u t) -> p g t u", t=PACK, u=4),
             )
 
-        def project(bank, w_words, w_scales, w_row, v_words, v_scales, v_row, a, j0):
+        def take_bank(number, shape):
+            return psum.tile(shape, F32, name="bank", tag="bank%d" % (number % BANKS))
+
+        def project(number, w_words, w_scales, v_words, v_scales, a, piece):
+            bank = take_bank(number, [P, PACK, PIECE])
+            j0 = piece * PIECE
             for t in range(PACK):
                 r_cols = slice(a * PASS + t * P, a * PASS + (t + 1) * P)
                 nc.tensor.matmul_mx(
                     out=bank[:, t, :],
                     lhsT=w_words[:, r_cols].bitcast(FP8X4),
-                    lhsT_scale=w_scales[w_row:P, r_cols],
+                    lhsT_scale=w_scales[:, r_cols],
                     rhs=v_words[j0 // HALF][:, j0 % HALF : j0 % HALF + PIECE].bitcast(FP8X4),
-                    rhs_scale=v_scales[v_row:P, j0 : j0 + PIECE],
+                    rhs_scale=v_scales[:, j0 : j0 + PIECE],
                     start=True,
                     stop=True,
                 )
+            return bank[:].rearrange("p t j -> p j t")
 
-        def take_bank(number, shape):
-            return psum.tile(shape, F32, name="bank", tag="bank%d" % (number % BANKS))
-
-        hb = keep.tile([P, J // PIECE, R_PASSES, PIECE, PACK], F32, name="hb", align_bytes=64)
+        hb = keep.tile([P, PIECES, R_PASSES, PIECE, PACK], F32, name="hb", align_bytes=64)
         for a in range(R_PASSES):
-            for piece in range(J // PIECE):
-                bank = take_bank(piece if a == 0 else piece % (BANKS // 2), [P, PACK, PIECE])
-                project(bank, wb_w, wb_s, 0, vb_w, vb_s, 0, a, piece * PIECE)
-                if a == 1 and piece in VECTOR_PIECES:
-                    nc.vector.tensor_copy(out=hb[:, piece, a], in_=bank[:].rearrange("p t j -> p j t"))
-                else:
-                    nc.scalar.copy(out=hb[:, piece, a], in_=bank[:].rearrange("p t j -> p j t"))
-        for half in range(2):
-            gather_words(va_w, tab_w, list_a, half)
+            for piece in range(PIECES):
+                sums = project(piece if a == 0 else piece % (BANKS // 2), wb_w, wb_s, vb_w, vb_s, a, piece)
+                evict = nc.vector.tensor_copy if (a, piece) == (1, 0) else nc.scalar.copy
+                evict(out=hb[:, piece, a], in_=sums)
+        gather_words(va_w, tab_w, list_a)
 
         firsts = [sum(CHUNKS[:c]) for c in range(len(CHUNKS))]
         h_bf, h_w, h_s = {}, {}, {}
@@ -175,10 +169,10 @@ def tile_list_kg_mul_sig_kernel(
             h_w[first] = keep.tile([P, R_PASSES, count * PIECE], U32, name="h_w%d" % first, align_bytes=64)
             h_s[first] = keep.tile([P, R_PASSES, count * PIECE], U8, name="h_s%d" % first, align_bytes=64)
         steps = [
-            (first, a * count + j, first + j, a)
+            (first, a * count + c, first + c, a)
             for first, count in zip(firsts, CHUNKS)
             for a in range(R_PASSES)
-            for j in range(count)
+            for c in range(count)
         ]
 
         def quantize_h(first, slot):
@@ -192,14 +186,11 @@ def tile_list_kg_mul_sig_kernel(
         def make_h(pair):
             for step in (2 * pair, 2 * pair + 1):
                 first, slot, piece, a = steps[step]
-                bank = take_bank(step + BANKS // 2, [P, PACK, PIECE])
-                project(bank, wa_w, wa_s, 0, va_w, va_s, 0, a, piece * PIECE)
-                nc.vector.tensor_tensor(
-                    h_bf[first][:, slot], bank[:].rearrange("p t j -> p j t"), hb[:, piece, a], MULT
-                )
+                sums = project(step + BANKS // 2, wa_w, wa_s, va_w, va_s, a, piece)
+                nc.vector.tensor_tensor(h_bf[first][:, slot], sums, hb[:, piece, a], MULT)
                 if step % 2 == 0 and step > 0:
                     quantize_h(*steps[step - 1][:2])
-            if pair == PIECES - 1:
+            if step == len(steps) - 1:
                 quantize_h(first, slot)
 
         out_tiles = out.rearrange("(g p) j -> p g j", p=P)
@@ -211,14 +202,14 @@ def tile_list_kg_mul_sig_kernel(
                 starts.append(N // P - 1)
             for b, (g0, g1) in enumerate(zip(starts, starts[1:] + [N // P])):
                 tiles = g1 - g0
-                bank = take_bank(R_PASSES * (first + 3) + b, [P, tiles, width])
+                bank = take_bank(2 * (first + 1) + BANKS // 2 + b, [P, tiles, width])
                 for g in range(tiles):
                     n_cols = slice((g0 + g) * P, (g0 + g + 1) * P)
                     for a in range(R_PASSES):
                         nc.tensor.matmul_mx(
                             out=bank[:, g, :],
                             lhsT=en_w[:, a, n_cols].bitcast(FP8X4),
-                            lhsT_scale=en_plane[:, a, n_cols],
+                            lhsT_scale=en_s[:, a, n_cols],
                             rhs=h_w[first][:, a, :].bitcast(FP8X4),
                             rhs_scale=h_s[first][:, a, :],
                             start=(a == 0),
@@ -227,11 +218,11 @@ def tile_list_kg_mul_sig_kernel(
                 result = keep.tile([P, tiles, width], F32, name="result%d_%d" % (first, g0))
                 nc.scalar.activation(result[:], bank[:], SIGMOID)
                 queries = slice(first * PIECE, first * PIECE + width)
-                nc.sync.dma_start(out=out_tiles[:, g0 : g0 + tiles, queries], in_=result[:])
+                nc.sync.dma_start(out=out_tiles[:, g0:g1, queries], in_=result[:])
 
-        for piece in range(LEAD):
-            make_h(piece)
+        for pair in range(LEAD):
+            make_h(pair)
         for c, (first, count) in enumerate(zip(firsts, CHUNKS)):
             score(first, count)
-            if c + LEAD < PIECES:
+            if c + LEAD < len(steps) // 2:
                 make_h(c + LEAD)

@@ -31,6 +31,7 @@ SPREAD_FIRST, SPREAD_STEP = 32, 4
 SPREAD_END = SPREAD_FIRST + SPREAD_STEP * SCALE_ROWS
 CHUNKS = [1, 1, 2, 2, 2]
 LEAD = BANKS // R_PASSES + 1
+VECTOR_BANKS = 2
 
 
 def as_words(codes):
@@ -56,7 +57,7 @@ def tile_list_kg_mul_sig_kernel(
         tab_s = keep.tile([P, T // 4], I32, name="tab_s", align_bytes=64)
         tab2_s = keep.tile([P, T // 4], I32, name="tab2_s", align_bytes=64)
         wa_raw_s = keep.tile([P, R // 4], I32, name="wa_raw_s", align_bytes=64)
-        wa_raw_w = keep.tile([P, R], I32, name="wa_raw_w", align_bytes=64)
+        wa_raw_w = [keep.tile([P, PASS], I32, name="wa_raw_w%d" % a, align_bytes=64) for a in range(R_PASSES)]
         tab_w = keep.tile([P, T], I32, name="tab_w", align_bytes=64)
         tab2_w = keep.tile([P, T], I32, name="tab2_w", align_bytes=64)
         staged_a = keep.tile([P, J + R + R_PASSES * N], U8, name="staged_a", align_bytes=64)
@@ -89,8 +90,9 @@ def tile_list_kg_mul_sig_kernel(
         nc.vector.tensor_copy(picked_b[:], tab2_s[:].bitcast(U8).indirect(list_b[:]))
         move_scale_rows(nc, plane_b, picked_b)
         nc.sync.dma_start(out=wb_raw[1][:], in_=wb_rows[:, :, passes[1]])
-        nc.sync.dma_start(out=wa_raw_w[:], in_=as_words(wa_words[0]))
         nc.sync.dma_start(out=tab_w[:], in_=as_words(tab_words[0]))
+        nc.sync.dma_start(out=wa_raw_w[0][:], in_=as_words(wa_words[0])[:, passes[0]])
+        nc.sync.dma_start(out=wa_raw_w[1][:], in_=as_words(wa_words[0])[:, passes[1]])
 
         va_w = [keep.tile([P, HALF], U32, name="va_w%d" % half, align_bytes=64) for half in range(2)]
         vb_w = [keep.tile([P, HALF], U32, name="vb_w%d" % half, align_bytes=64) for half in range(2)]
@@ -105,7 +107,7 @@ def tile_list_kg_mul_sig_kernel(
         wb_w = keep.tile([P, R], U32, name="wb_w", align_bytes=64)
         wb_s = keep.tile([P, R], U8, name="wb_s", align_bytes=64)
         for a, round_copy in enumerate((nc.scalar.copy, nc.vector.tensor_copy)):
-            wb_bf = keep.tile([P, PASS * PACK], BF16, name="wb_bf%d" % a, align_bytes=64)
+            wb_bf = keep.tile([P, PASS * PACK], BF16, name="wb_bf%d" % a, tag="wb_bf%d" % a, align_bytes=64)
             round_copy(
                 out=wb_bf[:].rearrange("p (t m i) -> p m t i", t=PACK, i=PACK),
                 in_=wb_raw[a][:].rearrange("p i (m t) -> p m t i", t=PACK),
@@ -128,11 +130,11 @@ def tile_list_kg_mul_sig_kernel(
         en_s = plane_bytes[:, J + R :].rearrange("p (a n) -> p a n", a=R_PASSES)
         vb_s = plane_b[:].bitcast(U8)
 
-        wa_w = keep.tile([P, R], I32, name="wa_w", align_bytes=64)
-        for cols in passes:
-            nc.vector.tensor_copy(
-                out=wa_w[:, cols].rearrange("p (t g u) -> p g t u", t=PACK, u=4),
-                in_=wa_raw_w[:, cols].rearrange("p (g u t) -> p g t u", t=PACK, u=4),
+        wa_w = [keep.tile([P, PASS], I32, name="wa_w%d" % a, align_bytes=64) for a in range(R_PASSES)]
+        for ordered, raw in zip(wa_w, wa_raw_w):
+            nc.gpsimd.tensor_copy(
+                out=ordered[:].rearrange("p (t g u) -> p g t u", t=PACK, u=4),
+                in_=raw[:].rearrange("p (g u t) -> p g t u", t=PACK, u=4),
             )
 
         def take_bank(number, shape):
@@ -145,7 +147,7 @@ def tile_list_kg_mul_sig_kernel(
                 r_cols = slice(a * PASS + t * P, a * PASS + (t + 1) * P)
                 nc.tensor.matmul_mx(
                     out=bank[:, t, :],
-                    lhsT=w_words[:, r_cols].bitcast(FP8X4),
+                    lhsT=w_words[a][:, t * P : (t + 1) * P].bitcast(FP8X4),
                     lhsT_scale=w_scales[:, r_cols],
                     rhs=v_words[j0 // HALF][:, j0 % HALF : j0 % HALF + PIECE].bitcast(FP8X4),
                     rhs_scale=v_scales[:, j0 : j0 + PIECE],
@@ -155,11 +157,17 @@ def tile_list_kg_mul_sig_kernel(
             return bank[:].rearrange("p t j -> p j t")
 
         hb = keep.tile([P, PIECES, R_PASSES, PIECE, PACK], F32, name="hb", align_bytes=64)
+        hb_vector = keep.tile([P, VECTOR_BANKS, PIECE, PACK], F32, name="hb_vector", tag="wb_bf1", align_bytes=64)
+
+        def hb_of(piece, a):
+            late = piece - (PIECES - VECTOR_BANKS)
+            return hb_vector[:, late] if a == 0 and late >= 0 else hb[:, piece, a]
+
         for a in range(R_PASSES):
             for piece in range(PIECES):
-                sums = project(piece if a == 0 else piece % (BANKS // 2), wb_w, wb_s, vb_w, vb_s, a, piece)
-                evict = nc.vector.tensor_copy if (a, piece) == (1, 0) else nc.scalar.copy
-                evict(out=hb[:, piece, a], in_=sums)
+                sums = project(piece, [wb_w[:, cols] for cols in passes], wb_s, vb_w, vb_s, a, piece)
+                evict = nc.vector.tensor_copy if a == 0 and piece >= PIECES - VECTOR_BANKS else nc.scalar.copy
+                evict(out=hb_of(piece, a), in_=sums)
         gather_words(va_w, tab_w, list_a)
 
         firsts = [sum(CHUNKS[:c]) for c in range(len(CHUNKS))]
@@ -186,8 +194,8 @@ def tile_list_kg_mul_sig_kernel(
         def make_h(pair):
             for step in (2 * pair, 2 * pair + 1):
                 first, slot, piece, a = steps[step]
-                sums = project(step + BANKS // 2, wa_w, wa_s, va_w, va_s, a, piece)
-                nc.vector.tensor_tensor(h_bf[first][:, slot], sums, hb[:, piece, a], MULT)
+                sums = project(step, wa_w, wa_s, va_w, va_s, a, piece)
+                nc.vector.tensor_tensor(h_bf[first][:, slot], sums, hb_of(piece, a), MULT)
                 if step % 2 == 0 and step > 0:
                     quantize_h(*steps[step - 1][:2])
             if step == len(steps) - 1:
@@ -202,7 +210,7 @@ def tile_list_kg_mul_sig_kernel(
                 starts.append(N // P - 1)
             for b, (g0, g1) in enumerate(zip(starts, starts[1:] + [N // P])):
                 tiles = g1 - g0
-                bank = take_bank(2 * (first + 1) + BANKS // 2 + b, [P, tiles, width])
+                bank = take_bank(2 * (first + 1) + b, [P, tiles, width])
                 for g in range(tiles):
                     n_cols = slice((g0 + g) * P, (g0 + g + 1) * P)
                     for a in range(R_PASSES):

@@ -60,8 +60,8 @@ def tile_list_kg_mul_sig_kernel(
         wa_raw_w = [keep.tile([P, PASS], I32, name="wa_raw_w%d" % a, align_bytes=64) for a in range(R_PASSES)]
         tab_w = keep.tile([P, T], I32, name="tab_w", align_bytes=64)
         tab2_w = keep.tile([P, T], I32, name="tab2_w", align_bytes=64)
-        staged_a = keep.tile([P, J + R + R_PASSES * N], U8, name="staged_a", align_bytes=64)
-        planes_a = keep.tile([P, (J + R + R_PASSES * N) // 4], I32, name="planes_a", align_bytes=64)
+        staged_a = keep.tile([P, J + R], U8, name="staged_a", align_bytes=64)
+        planes_a = keep.tile([P, (J + R) // 4], I32, name="planes_a", align_bytes=64)
         plane_b = keep.tile([P, J // 4], I32, name="plane_b", align_bytes=64)
         en_w = keep.tile([P, R_PASSES, N], I32, name="en_w", align_bytes=64)
         passes = [slice(a * PASS, (a + 1) * PASS) for a in range(R_PASSES)]
@@ -80,10 +80,6 @@ def tile_list_kg_mul_sig_kernel(
         nc.sync.dma_start(out=tab_s[spread, :], in_=tab_scales[0].bitcast(I32))
         nc.sync.dma_start(out=wa_raw_s[spread, :], in_=wa_scales[0].bitcast(I32))
         nc.sync.dma_start(out=tab2_w[:], in_=as_words(tab2_words[0]))
-        nc.sync.dma_start(
-            out=staged_a[spread, J + R :].bitcast(I32).rearrange("q (a n) -> q a n", a=R_PASSES),
-            in_=en_scales.rearrange("a q n -> q a n").bitcast(I32),
-        )
 
         picked_a = keep.tile([P, J], U8, name="picked_a", align_bytes=64)
         picked_b = keep.tile([P, J], U8, name="picked_b", align_bytes=64)
@@ -127,7 +123,6 @@ def tile_list_kg_mul_sig_kernel(
             nc.sync.dma_start(out=en_w[:, :, n0 : n0 + N // 2], in_=en_view[:, :, n0 : n0 + N // 2])
         plane_bytes = planes_a[:].bitcast(U8)
         va_s, wa_s = plane_bytes[:, :J], plane_bytes[:, J : J + R]
-        en_s = plane_bytes[:, J + R :].rearrange("p (a n) -> p a n", a=R_PASSES)
         vb_s = plane_b[:].bitcast(U8)
 
         wa_w = [keep.tile([P, PASS], I32, name="wa_w%d" % a, align_bytes=64) for a in range(R_PASSES)]
@@ -168,6 +163,12 @@ def tile_list_kg_mul_sig_kernel(
                 sums = project(piece, [wb_w[:, cols] for cols in passes], wb_s, vb_w, vb_s, a, piece)
                 evict = nc.vector.tensor_copy if a == 0 and piece >= PIECES - VECTOR_BANKS else nc.scalar.copy
                 evict(out=hb_of(piece, a), in_=sums)
+        for quadrant in range(P // QUADRANT):
+            p0, q0 = QUADRANT * quadrant + PACK, PACK * quadrant
+            nc.scalar.dma_start(
+                out=plane_b[p0 : p0 + R_PASSES * PACK, :], in_=en_scales[:, q0 : q0 + PACK, :].bitcast(I32)
+            )
+        en_s = [plane_b[PACK * (a + 1) :, :].bitcast(U8) for a in range(R_PASSES)]
         gather_words(va_w, tab_w, list_a)
 
         firsts = [sum(CHUNKS[:c]) for c in range(len(CHUNKS))]
@@ -217,7 +218,7 @@ def tile_list_kg_mul_sig_kernel(
                         nc.tensor.matmul_mx(
                             out=bank[:, g, :],
                             lhsT=en_w[:, a, n_cols].bitcast(FP8X4),
-                            lhsT_scale=en_s[:, a, n_cols],
+                            lhsT_scale=en_s[a][:, n_cols],
                             rhs=h_w[first][:, a, :].bitcast(FP8X4),
                             rhs_scale=h_s[first][:, a, :],
                             start=(a == 0),

@@ -29,7 +29,7 @@ BANK = 512
 BANKS = 8
 SPREAD_FIRST, SPREAD_STEP = 32, 4
 SPREAD_END = SPREAD_FIRST + SPREAD_STEP * SCALE_ROWS
-CHUNKS = [1, 1, 2, 2, 2]
+CHUNKS = [2, 2, 2, 2]
 LEAD = BANKS // R_PASSES + 1
 VECTOR_BANKS = 2
 
@@ -195,11 +195,11 @@ def tile_list_kg_mul_sig_kernel(
         def make_h(pair):
             for step in (2 * pair, 2 * pair + 1):
                 first, slot, piece, a = steps[step]
-                sums = project(step, wa_w, wa_s, va_w, va_s, a, piece)
+                number = step if step < BANKS else step % 2 + 6 * (pair % 2)
+                sums = project(number, wa_w, wa_s, va_w, va_s, a, piece)
                 nc.vector.tensor_tensor(h_bf[first][:, slot], sums, hb_of(piece, a), MULT)
-                if step % 2 == 0 and step > 0:
-                    quantize_h(*steps[step - 1][:2])
-            if step == len(steps) - 1:
+            if pair % 2:
+                quantize_h(first, slot - 2)
                 quantize_h(first, slot)
 
         out_tiles = out.rearrange("(g p) j -> p g j", p=P)
@@ -211,7 +211,7 @@ def tile_list_kg_mul_sig_kernel(
                 starts.append(N // P - 1)
             for b, (g0, g1) in enumerate(zip(starts, starts[1:] + [N // P])):
                 tiles = g1 - g0
-                bank = take_bank(2 * (first + 1) + b, [P, tiles, width])
+                bank = take_bank((0, 1, 2, 3, 4)[b] if first + count == PIECES else 2 + b, [P, tiles, width])
                 for g in range(tiles):
                     n_cols = slice((g0 + g) * P, (g0 + g + 1) * P)
                     for a in range(R_PASSES):
@@ -233,5 +233,5 @@ def tile_list_kg_mul_sig_kernel(
             make_h(pair)
         for c, (first, count) in enumerate(zip(firsts, CHUNKS)):
             score(first, count)
-            if c + LEAD < len(steps) // 2:
-                make_h(c + LEAD)
+            for pair in {0: [5], 1: [6, 7]}.get(c, []):
+                make_h(pair)

@@ -38,8 +38,8 @@ def as_words(codes):
     return codes.rearrange("p n i -> p (n i)").bitcast(I32)
 
 
-def move_scale_rows(nc, plane, spread_rows):
-    for r in range(PACK):
+def move_scale_rows(nc, plane, spread_rows, which=range(PACK)):
+    for r in which:
         rows = slice(SPREAD_FIRST + SPREAD_STEP * r, SPREAD_END, SPREAD_STEP * PACK)
         nc.sync.dma_start(out=plane[r:P:QUADRANT, :], in_=spread_rows[rows, :].bitcast(I32))
 
@@ -88,7 +88,6 @@ def tile_list_kg_mul_sig_kernel(
         nc.sync.dma_start(out=wb_raw[1][:], in_=wb_rows[:, :, passes[1]])
         nc.sync.dma_start(out=tab_w[:], in_=as_words(tab_words[0]))
         nc.sync.dma_start(out=wa_raw_w[0][:], in_=as_words(wa_words[0])[:, passes[0]])
-        nc.sync.dma_start(out=wa_raw_w[1][:], in_=as_words(wa_words[0])[:, passes[1]])
 
         va_w = [keep.tile([P, HALF], U32, name="va_w%d" % half, align_bytes=64) for half in range(2)]
         vb_w = [keep.tile([P, HALF], U32, name="vb_w%d" % half, align_bytes=64) for half in range(2)]
@@ -117,7 +116,9 @@ def tile_list_kg_mul_sig_kernel(
                 in_=wa_raw_s[:].bitcast(U8)[:, cols].rearrange("p (m t) -> p t m", t=PACK),
             )
         nc.vector.tensor_copy(staged_a[:, :J].bitcast(I32), picked_a[:].bitcast(I32))
-        move_scale_rows(nc, planes_a, staged_a)
+        move_scale_rows(nc, planes_a, staged_a, range(PACK // 2))
+        nc.sync.dma_start(out=wa_raw_w[1][:], in_=as_words(wa_words[0])[:, passes[1]])
+        move_scale_rows(nc, planes_a, staged_a, range(PACK // 2, PACK))
         en_view = en_words.rearrange("a p n i -> p a (n i)").bitcast(I32)
         for n0 in range(0, N, N // 2):
             nc.sync.dma_start(out=en_w[:, :, n0 : n0 + N // 2], in_=en_view[:, :, n0 : n0 + N // 2])
@@ -204,7 +205,7 @@ def tile_list_kg_mul_sig_kernel(
 
         out_tiles = out.rearrange("(g p) j -> p g j", p=P)
 
-        def score(first, count):
+        def score(first, count, between=()):
             width = count * PIECE
             starts = list(range(0, N // P, BANK // width))
             if first + count == PIECES:
@@ -228,10 +229,13 @@ def tile_list_kg_mul_sig_kernel(
                 nc.scalar.activation(result[:], bank[:], SIGMOID)
                 queries = slice(first * PIECE, first * PIECE + width)
                 nc.sync.dma_start(out=out_tiles[:, g0:g1, queries], in_=result[:])
+                if b == 0:
+                    for pair in between:
+                        make_h(pair)
 
         for pair in range(LEAD):
             make_h(pair)
         for c, (first, count) in enumerate(zip(firsts, CHUNKS)):
-            score(first, count)
-            for pair in {0: [5], 1: [6, 7]}.get(c, []):
+            score(first, count, [7] if c == 2 else [])
+            for pair in {0: [5], 1: [6]}.get(c, []):
                 make_h(pair)

@@ -70,6 +70,10 @@ def tile_list_kg_mul_sig_kernel(
         for tile in (tab2_s, tab_s, wa_raw_s, plane_b, planes_a):
             nc.vector.memset(tile[:], 0)
 
+        warm = keep.tile([P, 2, 32], F32, name="warm", align_bytes=64)
+        nc.vector.memset(warm[:, 0], 0.0)
+        nc.scalar.activation(warm[:, 1], warm[:, 0], SIGMOID)
+
         spread = slice(SPREAD_FIRST, SPREAD_END, SPREAD_STEP)
         wb_rows = wb.rearrange("(p i) r -> p i r", i=PACK)
         nc.sync.dma_start(out=wb_raw[0][:, : PACK // 2], in_=wb_rows[:, : PACK // 2, passes[0]])

from contextlib import ExitStack

import concourse.mybir as mybir

K, L, R, N, T, J = 512, 512, 1024, 1024, 4096, 1024
FLOPS = 2 * J * (K * R + L * R + R * N)

F32 = mybir.dt.float32
BF16 = mybir.dt.bfloat16
I32 = mybir.dt.int32
U32 = mybir.dt.uint32
U16 = mybir.dt.uint16
U8 = mybir.dt.uint8
FP8X4 = mybir.dt.float8_e4m3fn_x4
MULT = mybir.AluOpType.mult
SIGMOID = mybir.ActivationFunctionType.Sigmoid

P = 128
PACK = 4
PASS = P * PACK
R_PASSES = R // PASS
QUADRANT = 32
SCALE_ROWS = P // 8
LIST_GROUP = 16
HALF = J // 2
PIECE = P
PIECES = J // PIECE
BANK = 512
BANKS = 8
SPREAD_FIRST, SPREAD_STEP = 32, 4
SPREAD_END = SPREAD_FIRST + SPREAD_STEP * SCALE_ROWS
CHUNKS = [2, 2, 2, 2]
LEAD = BANKS // R_PASSES + 1
VECTOR_BANKS = 2


def as_words(codes):
    return codes.rearrange("p n i -> p (n i)").bitcast(I32)


def move_scale_rows(nc, plane, spread_rows, which=range(PACK)):
    for r in which:
        rows = slice(SPREAD_FIRST + SPREAD_STEP * r, SPREAD_END, SPREAD_STEP * PACK)
        nc.sync.dma_start(out=plane[r:P:QUADRANT, :], in_=spread_rows[rows, :].bitcast(I32))


def tile_list_kg_mul_sig_kernel(
    tc, tab_words, tab_scales, tab2_words, tab2_scales, wa_words, wa_scales, wb, en_words, en_scales, offs, offs2, out
):
    nc = tc.nc
    with ExitStack() as ctx:
        keep = ctx.enter_context(tc.tile_pool(name="keep", bufs=1))
        psum = ctx.enter_context(tc.psum_pool(name="psum", bufs=1))

        list_a = keep.tile([P, J // LIST_GROUP], U16, name="list_a")
        list_b = keep.tile([P, J // LIST_GROUP], U16, name="list_b")
        tab_s = keep.tile([P, T // 4], I32, name="tab_s", align_bytes=64)
        tab2_s = keep.tile([P, T // 4], I32, name="tab2_s", align_bytes=64)
        wa_raw_s = keep.tile([P, R // 4], I32, name="wa_raw_s", align_bytes=64)
        wa_raw_w = [keep.tile([P, PASS], I32, name="wa_raw_w%d" % a, align_bytes=64) for a in range(R_PASSES)]
        tab_w = keep.tile([P, T], I32, name="tab_w", align_bytes=64)
        tab2_w = keep.tile([P, T], I32, name="tab2_w", align_bytes=64)
        staged_a = keep.tile([P, J + R], U8, name="staged_a", align_bytes=64)
        planes_a = keep.tile([P, (J + R) // 4], I32, name="planes_a", align_bytes=64)
        plane_b = keep.tile([P, J // 4], I32, name="plane_b", align_bytes=64)
        en_w = keep.tile([P, R_PASSES, N], I32, name="en_w", align_bytes=64)
        passes = [slice(a * PASS, (a + 1) * PASS) for a in range(R_PASSES)]
        wb_raw = [keep.tile([P, PACK, PASS], F32, name="wb_raw%d" % a, align_bytes=64) for a in range(R_PASSES)]

        for tile in (tab2_s, tab_s, wa_raw_s, plane_b, planes_a):
            nc.vector.memset(tile[:], 0)

        warm = keep.tile([P, 2, 32], F32, name="warm", align_bytes=64)
        nc.vector.memset(warm[:, 0], 0.0)
        nc.scalar.activation(warm[:, 1], warm[:, 0], SIGMOID)

        spread = slice(SPREAD_FIRST, SPREAD_END, SPREAD_STEP)
        wb_rows = wb.rearrange("(p i) r -> p i r", i=PACK)
        nc.sync.dma_start(out=wb_raw[0][:, : PACK // 2], in_=wb_rows[:, : PACK // 2, passes[0]])
        nc.sync.dma_start(list_b[:], offs2)
        nc.sync.dma_start(list_a[:], offs)
        nc.sync.dma_start(out=tab2_s[spread, :], in_=tab2_scales[0].bitcast(I32))
        nc.sync.dma_start(out=wb_raw[0][:, PACK // 2 :], in_=wb_rows[:, PACK // 2 :, passes[0]])
        nc.sync.dma_start(out=tab_s[spread, :], in_=tab_scales[0].bitcast(I32))
        nc.sync.dma_start(out=wa_raw_s[spread, :], in_=wa_scales[0].bitcast(I32))
        nc.sync.dma_start(out=tab2_w[:], in_=as_words(tab2_words[0]))

        picked_a = keep.tile([P, J], U8, name="picked_a", align_bytes=64)
        picked_b = keep.tile([P, J], U8, name="picked_b", align_bytes=64)
        nc.vector.tensor_copy(picked_b[:], tab2_s[:].bitcast(U8).indirect(list_b[:]))
        move_scale_rows(nc, plane_b, picked_b)
        nc.sync.dma_start(out=wb_raw[1][:], in_=wb_rows[:, :, passes[1]])
        nc.sync.dma_start(out=tab_w[:], in_=as_words(tab_words[0]))
        nc.sync.dma_start(out=wa_raw_w[0][:], in_=as_words(wa_words[0])[:, passes[0]])

        va_w = [keep.tile([P, HALF], U32, name="va_w%d" % half, align_bytes=64) for half in range(2)]
        vb_w = [keep.tile([P, HALF], U32, name="vb_w%d" % half, align_bytes=64) for half in range(2)]

        def gather_words(picked, table, offsets):
            for half in range(2):
                entries = offsets[:, half * HALF // LIST_GROUP : (half + 1) * HALF // LIST_GROUP]
                nc.vector.tensor_copy(picked[half][:], table[:].bitcast(U32).indirect(entries))

        gather_words(vb_w, tab2_w, list_b)

        wb_w = keep.tile([P, R], U32, name="wb_w", align_bytes=64)
        wb_s = keep.tile([P, R], U8, name="wb_s", align_bytes=64)
        for a, round_copy in enumerate((nc.scalar.copy, nc.vector.tensor_copy)):
            wb_bf = keep.tile([P, PASS * PACK], BF16, name="wb_bf%d" % a, tag="wb_bf%d" % a, align_bytes=64)
            round_copy(
                out=wb_bf[:].rearrange("p (t m i) -> p m t i", t=PACK, i=PACK),
                in_=wb_raw[a][:].rearrange("p i (m t) -> p m t i", t=PACK),
            )
            nc.vector.quantize_mx(out=wb_w[:, passes[a]].bitcast(FP8X4), scales=wb_s[:, passes[a]], in_=wb_bf[:])

        nc.vector.tensor_copy(picked_a[:], tab_s[:].bitcast(U8).indirect(list_a[:]))
        for cols in passes:
            nc.vector.tensor_copy(
                out=staged_a[:, J : J + R][:, cols].rearrange("p (t m) -> p t m", t=PACK),
                in_=wa_raw_s[:].bitcast(U8)[:, cols].rearrange("p (m t) -> p t m", t=PACK),
            )
        nc.vector.tensor_copy(staged_a[:, :J].bitcast(I32), picked_a[:].bitcast(I32))
        move_scale_rows(nc, planes_a, staged_a, range(PACK // 2))
        nc.sync.dma_start(out=wa_raw_w[1][:], in_=as_words(wa_words[0])[:, passes[1]])
        move_scale_rows(nc, planes_a, staged_a, range(PACK // 2, PACK))
        en_view = en_words.rearrange("a p n i -> p a (n i)").bitcast(I32)
        for n0 in range(0, N, N // 2):
            nc.sync.dma_start(out=en_w[:, :, n0 : n0 + N // 2], in_=en_view[:, :, n0 : n0 + N // 2])
        plane_bytes = planes_a[:].bitcast(U8)
        va_s, wa_s = plane_bytes[:, :J], plane_bytes[:, J : J + R]
        vb_s = plane_b[:].bitcast(U8)

        wa_w = [keep.tile([P, PASS], I32, name="wa_w%d" % a, align_bytes=64) for a in range(R_PASSES)]
        for ordered, raw in zip(wa_w, wa_raw_w):
            nc.gpsimd.tensor_copy(
                out=ordered[:].rearrange("p (t g u) -> p g t u", t=PACK, u=4),
                in_=raw[:].rearrange("p (g u t) -> p g t u", t=PACK, u=4),
            )

        def take_bank(number, shape):
            return psum.tile(shape, F32, name="bank", tag="bank%d" % (number % BANKS))

        def project(number, w_words, w_scales, v_words, v_scales, a, piece):
            bank = take_bank(number, [P, PACK, PIECE])
            j0 = piece * PIECE
            for t in range(PACK):
                r_cols = slice(a * PASS + t * P, a * PASS + (t + 1) * P)
                nc.tensor.matmul_mx(
                    out=bank[:, t, :],
                    lhsT=w_words[a][:, t * P : (t + 1) * P].bitcast(FP8X4),
                    lhsT_scale=w_scales[:, r_cols],
                    rhs=v_words[j0 // HALF][:, j0 % HALF : j0 % HALF + PIECE].bitcast(FP8X4),
                    rhs_scale=v_scales[:, j0 : j0 + PIECE],
                    start=True,
                    stop=True,
                )
            return bank[:].rearrange("p t j -> p j t")

        hb = keep.tile([P, PIECES, R_PASSES, PIECE, PACK], F32, name="hb", align_bytes=64)
        hb_vector = keep.tile([P, VECTOR_BANKS, PIECE, PACK], F32, name="hb_vector", tag="wb_bf1", align_bytes=64)

        def hb_of(piece, a):
            late = piece - (PIECES - VECTOR_BANKS)
            return hb_vector[:, late] if a == 0 and late >= 0 else hb[:, piece, a]

        for a in range(R_PASSES):
            for piece in range(PIECES):
                sums = project(piece, [wb_w[:, cols] for cols in passes], wb_s, vb_w, vb_s, a, piece)
                evict = nc.vector.tensor_copy if a == 0 and piece >= PIECES - VECTOR_BANKS else nc.scalar.copy
                evict(out=hb_of(piece, a), in_=sums)
        for quadrant in range(P // QUADRANT):
            p0, q0 = QUADRANT * quadrant + PACK, PACK * quadrant
            nc.scalar.dma_start(
                out=plane_b[p0 : p0 + R_PASSES * PACK, :], in_=en_scales[:, q0 : q0 + PACK, :].bitcast(I32)
            )
        en_s = [plane_b[PACK * (a + 1) :, :].bitcast(U8) for a in range(R_PASSES)]
        gather_words(va_w, tab_w, list_a)

        firsts = [sum(CHUNKS[:c]) for c in range(len(CHUNKS))]
        h_bf, h_w, h_s = {}, {}, {}
        for first, count in zip(firsts, CHUNKS):
            h_bf[first] = keep.tile([P, R_PASSES * count, PIECE, PACK], BF16, name="h_bf%d" % first, align_bytes=64)
            h_w[first] = keep.tile([P, R_PASSES, count * PIECE], U32, name="h_w%d" % first, align_bytes=64)
            h_s[first] = keep.tile([P, R_PASSES, count * PIECE], U8, name="h_s%d" % first, align_bytes=64)
        steps = [
            (first, a * count + c, first + c, a)
            for first, count in zip(firsts, CHUNKS)
            for a in range(R_PASSES)
            for c in range(count)
        ]

        def quantize_h(first, slot):
            cols = slice((slot - 1) * PIECE, (slot + 1) * PIECE)
            nc.vector.quantize_mx(
                out=h_w[first][:].rearrange("p a j -> p (a j)")[:, cols].bitcast(FP8X4),
                scales=h_s[first][:].rearrange("p a j -> p (a j)")[:, cols],
                in_=h_bf[first][:, slot - 1 : slot + 1].rearrange("p s j t -> p (s j t)"),
            )

        def make_h(pair):
            for step in (2 * pair, 2 * pair + 1):
                first, slot, piece, a = steps[step]
                number = step if step < BANKS else step % 2 + 6 * (pair % 2)
                sums = project(number, wa_w, wa_s, va_w, va_s, a, piece)
                nc.vector.tensor_tensor(h_bf[first][:, slot], sums, hb_of(piece, a), MULT)
            if pair % 2:
                quantize_h(first, slot - 2)
                quantize_h(first, slot)

        out_tiles = out.rearrange("(g p) j -> p g j", p=P)

        def score(first, count, between=()):
            width = count * PIECE
            starts = list(range(0, N // P, BANK // width))
            if first + count == PIECES:
                starts.append(N // P - 1)
            for b, (g0, g1) in enumerate(zip(starts, starts[1:] + [N // P])):
                tiles = g1 - g0
                bank = take_bank((0, 1, 2, 3, 4)[b] if first + count == PIECES else 2 + b, [P, tiles, width])
                for g in range(tiles):
                    n_cols = slice((g0 + g) * P, (g0 + g + 1) * P)
                    for a in range(R_PASSES):
                        nc.tensor.matmul_mx(
                            out=bank[:, g, :],
                            lhsT=en_w[:, a, n_cols].bitcast(FP8X4),
                            lhsT_scale=en_s[a][:, n_cols],
                            rhs=h_w[first][:, a, :].bitcast(FP8X4),
                            rhs_scale=h_s[first][:, a, :],
                            start=(a == 0),
                            stop=(a == R_PASSES - 1),
                        )
                result = keep.tile([P, tiles, width], F32, name="result%d_%d" % (first, g0))
                nc.scalar.activation(result[:], bank[:], SIGMOID)
                queries = slice(first * PIECE, first * PIECE + width)
                nc.sync.dma_start(out=out_tiles[:, g0:g1, queries], in_=result[:])
                if b == 0:
                    for pair in between:
                        make_h(pair)

        for pair in range(LEAD):
            make_h(pair)
        for c, (first, count) in enumerate(zip(firsts, CHUNKS)):
            score(first, count, [7] if c == 2 else [])
            for pair in {0: [5], 1: [6]}.get(c, []):
                make_h(pair)
